import numpy as np, ml_dtypes
CORES = [10,34,74,98]
N = 4
import mx_ref
BF = ml_dtypes.bfloat16
def gcols(t, e):
    v = np.concatenate([t.reshape(8, 16, -1, 4), np.zeros((8, 16, 1, 4), BF)], axis=2)
    return np.ascontiguousarray(np.stack([v[g][:, e[g]] for g in range(8)])).reshape(128, -1)
def tile(rs):
    return np.stack(rs, axis=2).reshape(128, -1).astype(BF)
def pick(q, e):
    c = np.concatenate([q[0].reshape(128, -1, 4), np.zeros((128, 1, 4), np.uint8)], axis=1); s = np.concatenate([q[1], np.ones((16, 1), np.uint8)], axis=1)
    return (np.ascontiguousarray(c[:, e].reshape(128, -1)), np.ascontiguousarray(s[:, e]))
def join(*qs):
    return (np.concatenate([q[0] for q in qs], axis=1), np.concatenate([q[1] for q in qs], axis=1))
def put(q, e, v):
    c, s = q[0].reshape(128, -1, 4).copy(), q[1].copy(); c[:, e] = v[0].reshape(128, -1, 4); s[:, e] = v[1]
    return (c.reshape(128, -1), s)
def pk(c, s):
    return (np.ascontiguousarray(c), mx_ref.live(s))
def emit(q):
    return q[0], q[1]
def packed(v, rng):
    q = [mx_ref.quantize(np.ascontiguousarray(v[r])) for r in range(N)]
    return np.stack([a for a, b in q]), np.stack([mx_ref.plane(b, rng) for a, b in q])
def values_of_codes():
    e, c = np.zeros((128, 128, 4), np.float32), np.zeros((128, 2, 4), np.uint8)
    e[np.arange(128), np.arange(128), 0] = 1
    c[:127, :, 0] = np.arange(256).reshape(2, 128).T[:127]
    return mx_ref.matmul(mx_ref.quantize(e.reshape(128, 512).astype(BF)), (c.reshape(128, 8), np.full((16, 2), 127, np.uint8))).T.reshape(-1).astype(np.float64)
CODE_VALUE, SCALE_VALUE = values_of_codes(), 2.0 ** (np.arange(256) - 127.0)
def decode(q):
    return (CODE_VALUE[q[0]].reshape(16, 8, -1, 4) * SCALE_VALUE[q[1]][:, None, :, None] + 0.0).reshape(128, -1).astype(np.float32)
def f(rng, *shape):
    return mx_ref.flush((rng.standard_normal(shape, dtype=np.float32) * np.exp2(rng.integers(-2, 3, shape[:-1] + (1,)))).astype(BF))
def wide(rng, *shape, cols=0):
    v = rng.standard_normal(shape, dtype=np.float32) * np.exp2(rng.integers(-12, 13, shape)).astype(np.float32)
    if cols: v *= np.repeat(np.exp2(rng.integers(-cols, cols + 1, shape[:-2] + (1, shape[-1] // 4))) * (rng.random(shape[:-2] + (1, shape[-1] // 4)) > 0.0625), 4, axis=-1).astype(np.float32)
    return mx_ref.flush(v.astype(BF))
S, Z, E, C, A, R = 18, 16, 8, 288, 144, 3
DEPTH = np.arange(E)
AWAY = np.abs(np.arange(S)[:, None] - np.arange(S))
CONE = DEPTH[:, None, None] - AWAY[:, None, :, None] >= DEPTH
def cuts(p):
    rich = (p[::16] > 0).reshape(8, S, Z)[:, :, :E]
    good = 2 * np.sum(rich[:, None, None] & CONE, axis=(3, 4)) > np.sum(CONE, axis=(2, 3))
    return np.sum((good[:, :, :, None, None] & CONE).any(axis=(1, 2)), axis=2)
def slots(a):
    n = a[:, :, None]
    return np.where(DEPTH < n, Z * np.arange(S)[:, None] + n - 1 - DEPTH, -1).reshape(8, A)
def places(a, s):
    n, c, k = a[:, :, None], np.arange(S)[:, None], np.arange(Z)
    i = k - Z + n
    return np.where(i < 0, Z * c + k + n, np.where(i < s[:, :, None], C + E * c + i, Z * c + n - 1 - i)).reshape(8, C)
def big(v):
    v = v.astype(np.float32)
    v[np.abs(v) < np.float32(2.0 ** -16)] = 0
    return v.astype(BF)
def numbers_of(rng):
    return {"x": big(f(rng, N, 128, 4 * C)), "u": np.array(f(rng, N, 128, 512)), "v": np.array(f(rng, N, 128, 512))}
def weights(rng, still=[], fade=[]):
    w = big(f(rng, N, 128, 2048)).reshape(N, 8, 16, 4, 8, 16, 4)
    for i in still:
        w[:, :, i] = 0
        w[:, :, :, :, :, i] = 0
    for g in fade:
        w[:, g, 0, 0, g, 0, 0] = -64
        w[:, g, 0, 0, g, 1, 0] = 0.25
    c, p = packed(w.reshape(N, 128, 2048), rng)
    return {"wc": c, "ws": p}
def setup_inputs(rng):
    return {**numbers_of(rng), **weights(rng)}
def setup_inputs_zeros(rng):
    d = numbers_of(rng)
    x = d["x"].reshape(N, 8, 16, C, 4)
    x.transpose(0, 1, 3, 2, 4)[rng.permutation(N * 8 * C).reshape(N, 8, C) % 3 == 0] = 0
    for r in range(N): x[r][:, :, rng.permutation(C)[:C // 8]] = 0
    x[int(rng.integers(N))].reshape(8, 16, S, Z, 4)[:, :, :, :E] = 0
    return {"x": x.reshape(N, 128, 4 * C), "u": d["u"], "v": d["v"], **weights(rng)}
def setup_inputs_cones(rng):
    d = numbers_of(rng)
    x = d["x"].astype(np.float32).reshape(N, 8, 16, C, 4)
    u = d["u"].reshape(N, 128, 128, 4)
    x[:, :, :8] = 0
    u[:, :, ::16] = 0
    c, k = np.arange(C) // Z, np.arange(C) % Z
    o = rng.permutation(8)
    low = int(o[2])
    size = np.where(rng.permutation(N) < N // 2, 2.0 ** -30, 1.0)
    for r in range(N):
        m, n = rng.integers(E + 1, S - E, 2)
        at = int(rng.integers(E, S - E))
        one = 2 * int(rng.integers(E // 2, (S - E) // 2)) + 1
        even = c % 2 == 0
        side = c < m if r % 2 else c >= n
        h = r // 2 % 2 * (E - 2)
        cone = (k + np.abs(c - (S - 1 - h if r % 2 else h)) < E)
        more = rng.permutation(np.flatnonzero(cone & ~side))
        side[more[:int(np.sum(cone)) // 2 + 1 - int(np.sum(cone & side))]] = True
        kinds = [even, ~even, side, k + np.abs(c - at) < E, even | (c == one) & (k == 0)]
        rich = np.zeros((8, C), bool)
        rich[o[r % 2]] = True
        rich[low] = (k <= 2 * E) | (k == Z - 1)
        for g, i in zip(o[3:], rng.permutation(5)): rich[g] = kinds[i]
        small = np.where(np.arange(8) == low, 2.0 ** -30, size[r])
        mark = np.where(rich, 1, -rng.integers(0, 2, (8, C))) * small[:, None]
        for g in rng.permutation(np.delete(o, 2))[:4]:
            j = int(rng.integers(C))
            mark[g, j] = 2.0 ** 30 if rich[g, j] else -2.0 ** 30
        x[r, :, 0, :, 0] = mark
        x[r, low, 7, :, 0] = 2.0 ** -30
        for g in range(8): u[r, 16 * g, 16 * g, 0] = small[g]
        u[r, 16 * low + 1, 16 * low, 0] = 2.0 ** -30
    return {"x": x.reshape(N, 128, 4 * C).astype(BF), "u": u.reshape(N, 128, 512), "v": d["v"], **weights(rng, range(8), [low])}
def setup_inputs_huge(rng):
    d = numbers_of(rng)
    x = 2.0 ** 30 * (0.8 + 0.2 * rng.random((N, 128, C, 4)))
    c = np.stack([rng.permutation(C) % 2 * 2.0 - 1.0 for r in range(N)])
    c[rng.permutation(N) < N // 2] = 1
    x *= c[:, None, :, None]
    u = d["u"].reshape(N, 128, 8, 16, 4)
    s = np.stack([rng.permutation(8) % 2 * 2.0 - 1.0 for r in range(N)])
    a = 2.0 ** 30 * (1 - 0.1 * rng.random((N, 128, 8, 4))) * s[:, None, :, None]
    u[:, :, :, 0] = a.astype(np.float32).astype(BF)
    w = np.zeros((N, 128, 4, 128, 4), np.float32)
    i = np.arange(128)
    for b in range(4): w[:, i, b, i, b] = -1
    wc, ws = packed(w.reshape(N, 128, 2048).astype(BF), rng)
    return {"x": x.astype(np.float32).reshape(N, 128, 4 * C).astype(BF), "u": u.reshape(N, 128, 512), "v": d["v"], "wc": wc, "ws": ws}
def setup_inputs_spread(rng):
    d = setup_inputs(rng)
    d["x"] = big(wide(rng, N, 128, 4 * C, cols=6))
    return d
def check_inputs(d):
    b = []
    for k in ("x", "u", "v"):
        a = np.abs(d[k].astype(np.float32))
        if not (np.isfinite(a).all() and ((a == 0) | (a >= 2.0 ** -30) & (a <= 2.0 ** 30)).all()): b.append("a value of " + k)
    if ((d["wc"] & 0x7F) == 0x7F).any(): b.append("a code of wc that is no number")
    z = np.zeros((128, 4, 4), np.float32)
    z[:, 1] = 2.0 ** -30
    z[:, 2] = 2.0 ** 30
    c, s = emit(mx_ref.quantize(z.reshape(128, 16).astype(BF)))
    for r in range(N):
        p = mx_ref.live(d["ws"][r])
        if not ((p == s[0, 0]) | (p >= s[0, 1]) & (p <= s[0, 2])).all(): b.append("a scale of ws")
    return b
def reference(x, u, v, wc, ws):
    qu = [mx_ref.quantize(u[r]) for r in range(N)]
    lay = [pk(wc[r], ws[r]) for r in range(N)]
    now = [x[r] for r in range(N)]
    a = []
    for t in range(R):
        a, held, sent = [], [], []
        for r in range(N):
            q = mx_ref.quantize(now[r])
            a.append(cuts(mx_ref.matmul(qu[r], q)))
            held.append(decode(q).astype(BF))
            sent.append(mx_ref.quantize(gcols(held[r], slots(a[r]))))
        for r in range(N):
            s = (r - 1 - t) % N
            d = decode(sent[s])
            h = tile([mx_ref.matmul(pick(lay[r], np.arange(128 * b, 128 * b + 128)), sent[s]) * np.float32(0.015625) + d[:, b::4] for b in range(4)])
            now[r] = gcols(np.concatenate([held[r], h], axis=1), places(a[r], a[s]))
    y, oa = np.zeros((N, 128, C), np.float32), np.zeros((N, 8, S), np.float32)
    oc, osc = np.zeros((N, 128, 4 * C), np.uint8), np.zeros((N, 16, C), np.uint8)
    for r in range(N):
        q = mx_ref.quantize(now[r])
        y[r] = mx_ref.matmul(mx_ref.quantize(v[r]), q)
        oa[r] = a[r]
        oc[r], osc[r] = emit(q)
    return {"y": y, "oa": oa, "oc": oc, "osc": osc}

@@ -1,0 +1,471 @@
+from concourse.bass import DstId, RemoteDMATransfer
+from concourse.mybir import dt, AluOpType, ActivationFunctionType
+
+BF, F32, I32, U16, FP, U8 = "bfloat16", "float32", "int32", "uint16", "float8_e4m3fn_x4", "uint8"
+SCRATCH = {"ps": ("psum", [128, 4096], F32)}
+for _n, _w in (("xb", 1152), ("ub", 512), ("vb", 512), ("src0", 1152), ("src1", 2320), ("src2", 1728), ("ts0", 1152),
+               ("ts2", 1152), ("x1t", 576), ("h0", 576), ("x2t", 576), ("x2b", 576), ("b0", 576), ("b1", 576),
+               ("b2", 576), ("x3", 1152), ("rich", 512), ("cone", 648), ("eb", 528), ("c64", 128),
+               ("icp", 180), ("dep", 162), ("ab", 648)):
+    SCRATCH[_n] = ("sbuf", [128, _w], BF)
+for _n, _w in (("u", 128), ("up", 128), ("v", 128), ("w", 512), ("e", 512), ("cone", 162), ("rich", 128), ("x0", 288),
+               ("t0", 144), ("l0", 144), ("d0", 144), ("x1t", 144), ("h0", 144), ("b0", 144), ("b1", 144), ("f0", 288),
+               ("l1", 144), ("x2t", 144), ("l2", 144), ("d2", 144), ("x2b", 144), ("b2", 144), ("x3", 288)):
+    SCRATCH["q_" + _n] = ("sbuf", [128, _w], FP)
+    SCRATCH["s_" + _n] = ("sbuf", [128, _w], U8)
+for _n, _w, _d in (("pi", 8, I32), ("pc", 24, F32), ("cc", 576, F32), ("ci", 576, F32), ("bi", 198, F32), ("bc", 198, F32),
+                   ("li", 64, I32), ("lf", 64, F32), ("lu", 40, U16), ("wf", 4000, F32), ("wi", 256, I32), ("off", 320, U16),
+                   ("o0", 36, U16), ("o2", 36, U16), ("lo0", 36, U16), ("lo2", 36, U16), ("a1", 36, I32),
+                   ("la1", 36, I32), ("oaf", 18, F32), ("yb", 288, F32)):
+    SCRATCH[_n] = ("sbuf", [128, _w], _d)
+
+SEMAPHORES = ["cv", "cs", "ct", "cg", "sent"] + ["dm%d" % i for i in range(16)] + ["ar%d" % i for i in range(10)]
+
+A = AluOpType
+ACT = ActivationFunctionType
+WIDE = {BF: 2, F32: 4, I32: 4, U16: 2, FP: 4, U8: 1}
+COST = {"cyc": 0.001, "gather": 1.56, "wake": 0.08, "pe": 0.00063, "call": 0.5, "far": 1.0, "row": 0.05, "byte": 0.00007, "first": 1.5}
+OPT = {"e_t0": "ssss", "e_f0": "ssss", "e_ts0": "vvss", "e_b1": "vs", "e_t2t": "ssss", "e_h1": "ssss", "e_x2b": "vs",
+       "e_ts2": "vvss", "e_t2b": "ssss", "b_t2t": 1, "b_t2b": 1, "b_f0": 0, "b_h1": 0, "b_ts2": 0, "vat": "o2"}
+ORDER = [0, 4, 32, 1, 2, 3, 7, 9, 6, 5, 8, 10, 34, 43, 21, 20, 11, 35, 36, 12, 29, 47, 30, 44, 48, 45, 23, 24, 17, 22, 161, 54, 173, 168, 51, 62, 52, 37, 31, 38, 49, 46, 55, 56, 73, 74, 59, 76, 13, 162, 16, 14, 28, 26, 27, 174, 25, 75, 15, 61, 60, 50, 94, 90, 78, 77, 79, 80, 95, 91, 63, 53, 81, 82, 57, 58, 83, 92, 96, 84, 93, 19, 97, 33, 85, 39, 86, 88, 87, 40, 98, 99, 100, 101, 102, 103, 116, 104, 105, 199, 171, 70, 89, 68, 205, 66, 72, 64, 176, 106, 119, 117, 107, 108, 41, 109, 169, 200, 120, 118, 123, 121, 201, 42, 110, 111, 112, 114, 113, 125, 160, 115, 163, 124, 177, 122, 71, 18, 126, 178, 164, 170, 165, 129, 133, 127, 131, 175, 166, 167, 134, 130, 128, 132, 136, 65, 210, 135, 172, 212, 211, 137, 139, 142, 143, 145, 148, 146, 140, 149, 180, 193, 179, 138, 181, 190, 182, 183, 197, 147, 141, 184, 144, 150, 151, 156, 154, 155, 158, 152, 159, 185, 191, 194, 157, 186, 189, 153, 192, 187, 188, 198, 213, 195, 206, 217, 196, 216, 219, 240, 242, 218, 202, 241, 67, 214, 215, 220, 246, 221, 203, 209, 207, 204, 222, 208, 223, 248, 243, 247, 228, 234, 229, 237, 238, 235, 231, 224, 249, 226, 225, 227, 250, 275, 232, 244, 251, 276, 230, 239, 236, 233, 69, 253, 273, 277, 245, 252, 279, 254, 255, 256, 267, 265, 266, 268, 257, 263, 261, 259, 278, 284, 280, 281, 258, 269, 271, 264, 260, 262, 301, 285, 286, 287, 288, 298, 289, 299, 290, 292, 293, 295, 296, 270, 272, 294, 300, 302, 282, 303, 274, 304, 283, 305, 291, 306, 297, 307, 308, 309, 311, 310, 312, 313, 317, 318, 316, 319, 315, 314, 320]
+
+
+def vw(name, a, b, step=1):
+    return (name, a, b, step)
+
+
+def cols(v):
+    return range(v[1], v[2], v[3])
+
+
+def plan(T, topo, core, rank, C=COST, O=OPT):
+    ops = []
+    cores = T.cores
+    n = len(cores)
+    CYC = C["cyc"]
+
+    def ap(v):
+        return T[v[0]][:, v[1]:v[2]:v[3]] if v[3] != 1 else T[v[0]][:, v[1]:v[2]]
+
+    def op(eng, dur, fn, reads, writes, kind="c", lat=0.0, acc=False):
+        ops.append({"eng": eng, "dur": dur, "fn": fn, "r": [v for v in reads if isinstance(v, tuple)], "w": list(writes),
+                    "kind": kind, "lat": lat, "acc": acc, "id": len(ops)})
+        return ops[-1]
+
+    def sc(x):
+        return ap(x) if isinstance(x, tuple) else x
+
+    def narrow(*vs):
+        return all(WIDE[SCRATCH[v[0]][2]] == 2 for v in vs)
+
+    def vdur(m, f=1.0):
+        return max(64, m * f) * CYC
+
+    def ts(out, in0, s1, op0, s2=None, op1=None):
+        d = vdur(len(cols(out)), 0.5 if narrow(out, in0) else 1.0)
+        if op1 is None:
+            return op("v", d, lambda q: q.tensor_scalar(ap(out), ap(in0), sc(s1), None, op0), [in0, s1], [out])
+        return op("v", d, lambda q: q.tensor_scalar(ap(out), ap(in0), sc(s1), sc(s2), op0, op1), [in0, s1, s2], [out])
+
+    def tt(out, a, b, o):
+        return op("v", vdur(len(cols(out)), 2.0), lambda q: q.tensor_tensor(ap(out), ap(a), ap(b), o), [a, b], [out])
+
+    def cp(out, a):
+        return op("v", vdur(len(cols(out))), lambda q: q.tensor_copy(ap(out), ap(a)), [a], [out])
+
+    def fill(out, val):
+        return op("v", vdur(len(cols(out)), 0.5 if narrow(out) else 1.0), lambda q: q.memset(ap(out), val), [], [out])
+
+    def scan(out, d0, d1, init, o0, o1):
+        return op("v", vdur(len(cols(out))), lambda q: q.tensor_tensor_scan(ap(out), ap(d0), ap(d1), init, o0, o1), [d0, d1], [out])
+
+    def act(out, a, func=None, bias=0.0, scale=1.0):
+        f = ACT.Identity if func is None else func
+        if f == ACT.Copy:
+            fn = lambda q: q.activation(ap(out), ap(a), f, scale=scale) if scale != 1.0 else q.activation(ap(out), ap(a), f)
+        else:
+            fn = lambda q: q.activation(ap(out), ap(a), f, bias=sc(bias), scale=scale)
+        return op("s", vdur(len(cols(out))), fn, [a, bias], [out])
+
+    def iota(out, pat, base, cm=0):
+        if SCRATCH[out[0]][2] != I32:
+            fn = lambda q: q.iota(ap(out), pat, base, cm, allow_small_or_imprecise_dtypes=True)
+        else:
+            fn = lambda q: q.iota(ap(out), pat, base, cm)
+        return op("g", (156 + 2 * len(cols(out))) * CYC, fn, [], [out])
+
+    def quant(name, src, a=0):
+        m = len(cols(src)) // 4
+        qv, sv = vw("q_" + name, a, a + m), vw("s_" + name, a, a + m)
+        return op("v", (15 + 1.06 * m) * CYC, lambda q: q.quantize_mx(ap(qv), ap(sv), ap(src)), [src], [qv, sv])
+
+    def mm(bank, lhs, la, rhs, ra, m, start=True, stop=True):
+        out = vw("ps", 512 * bank, 512 * bank + m)
+        lq, ls = vw("q_" + lhs, la, la + 128), vw("s_" + lhs, la, la + 128)
+        rq, rs = vw("q_" + rhs, ra, ra + m), vw("s_" + rhs, ra, ra + m)
+        return op("t", (m + 16) * C["pe"], lambda q: q.matmul_mx(ap(out), ap(lq), ap(ls), ap(rq), ap(rs), start, stop),
+                  [lq, ls, rq, rs], [out], acc=not start)
+
+    def gather(eng, out, win, offs):
+        d = (60 + len(cols(out)) * C["gather"]) * CYC
+        if eng == "v":
+            return op("v", d, lambda q: q.tensor_copy(ap(out), ap(win).indirect(ap(offs))), [win, offs], [out])
+        return op("s", d, lambda q: q.activation(ap(out), ap(win).indirect(ap(offs)), ACT.Copy), [win, offs], [out])
+
+    def gather2(out, win, offs, engs, o0=0):
+        for i, e in enumerate(engs):
+            gather(e, vw(out, 288 * i, 288 * i + 288), win, vw(offs, o0 + 18 * i, o0 + 18 * i + 18))
+
+    def pick(dst, src, w, offs):
+        m = 16 * len(cols(offs))
+        qo, so, qi, si = vw("q_" + dst, 0, m), vw("s_" + dst, 0, m), vw("q_" + src, 0, w), vw("s_" + src, 0, w)
+        d = (60 + m * C["gather"]) * CYC
+        op("v", d, lambda q: q.tensor_copy(ap(qo).bitcast(dt.uint32), ap(qi).bitcast(dt.uint32).indirect(ap(offs))), [qi, offs], [qo])
+        op("s", d, lambda q: q.activation(ap(so), ap(si).indirect(ap(offs)), ACT.Copy), [si, offs], [so])
+
+    def unpack(q, m, dst, d0, banks, engs, w=False):
+        for b in (0, 2, 1, 3):
+            if w:
+                mm(banks[b], "w", 128 * b, q, 0, m, True, False)
+            mm(banks[b], "e", 128 * b, q, 0, m, not w, True)
+            src, out = vw("ps", 512 * banks[b], 512 * banks[b] + m), vw(dst, d0 + b, d0 + 4 * m, 4)
+            if engs[b] == "v":
+                ts(out, src, 0.015625, A.mult)
+            else:
+                act(out, src, ACT.Copy, scale=0.015625)
+
+    def dma(eng, out, in_, reads, writes, nbytes):
+        o = op(eng, 0.1, lambda q: q.dma_start(out, in_), reads, writes, kind="d", lat=0.7)
+        o["pre"], o["wire"] = 1.3, (8 * C["row"] * 0.6 + nbytes / 16 * C["byte"] * 0.6 if nbytes else 0.05)
+
+    def send(t, pairs):
+        dst = cores[(rank + 1 + t) % n]
+        rid, pid = topo.addr(dst)[0], topo.addr(dst)[1]
+        eng = topo.engines(core, dst)
+        share = len(eng) // len(pairs)
+
+        def side(v):
+            return ap(v).bitcast(dt.uint8) if SCRATCH[v[0]][2] == FP else ap(v)
+
+        def fn(q, sem, sent):
+            if len(pairs) == 1:
+                return q.remote_dma(side(pairs[0][1]), side(pairs[0][0]), sem, sent, pid, rid, topo.mask(core, dst))
+            trs = []
+            for i, (s, d) in enumerate(pairs):
+                m = sum(1 << e for e in eng[share * i:share * i + share])
+                trs.append(RemoteDMATransfer(dst_ids=[DstId(rid=rid, pnc=pid)], dma_engine_mask=m, remote_sem=sem, src=side(s), dst=side(d)))
+            return q.remote_dma_fused(trs, local_sem=sent)
+        v = pairs[0][0]
+        o = op("g", C["call"], fn, [p[0] for p in pairs], [p[1] for p in pairs], kind="r", lat=C["far"])
+        o["n"], o["pre"] = share * len(pairs), 0.0
+        o["wire"] = 128 / share * (C["row"] + C["byte"] * len(cols(v)) * WIDE[SCRATCH[v[0]][2]])
+
+    nxt = {"wf": 2, "wi": 0, "off": 0, "ci": 0}
+
+    def new(buf, m=36):
+        nxt[buf] += m
+        return vw(buf, nxt[buf] - m, nxt[buf])
+
+    def step(v, h, s):
+        return vw(v[0], v[1] + h, v[2], s)
+
+    dma("y", T.xb[:], T.x[:], [], [vw("xb", 0, 1152)], 294912)
+    dma("y", T.ub[:], T.u[:], [], [vw("ub", 0, 512)], 131072)
+    dma("y", T.q_w[:].bitcast(dt.uint8), T.wc[:], [], [vw("q_w", 0, 512)], 262144)
+    dma("y", T.s_w[:], T.ws[:], [], [vw("s_w", 0, 512)], 65536)
+
+    P, R, R8, TT, I0, K7, C3, PEN, KH0, KH1, EX, EX8, T576, TM32, KB, NK0, NK1 = [vw("pc", i, i + 1) for i in range(17)]
+    p = vw("pi", 0, 1)
+    iota(p, [[0, 1]], 0, 1)
+    ts(vw("pi", 1, 2), p, 15, A.bitwise_and)
+    ts(vw("pi", 2, 3), p, 8, A.bitwise_and)
+    ts(vw("pi", 3, 4), p, 3, A.bitwise_and)
+    ts(vw("pi", 4, 5), p, 12, A.bitwise_and, 2, A.logical_shift_right)
+    ts(vw("pi", 5, 6), p, 7, A.bitwise_and)
+    ts(vw("pi", 6, 7), p, 3, A.logical_shift_right)
+    cp(vw("pc", 0, 7), vw("pi", 0, 7))
+    ts(PEN, p, 112.0, A.is_lt, 1000.0, A.mult)
+    act(KB, I0, scale=-72.0, bias=TT)
+    act(KH0, KB, bias=504.0)
+    act(KH1, KB, bias=216.0)
+    act(EX, KB, scale=-1.0 / 72, bias=-3.472)
+    act(T576, TT, bias=576.0)
+    act(EX8, KB, scale=-1.0 / 72, bias=-11.472)
+    act(TM32, TT, bias=-32.0)
+    fill(vw("c64", 0, 128), 64.0)
+    iota(vw("dep", 0, 162), [[0, 18], [1, 9]], -1)
+    for b in range(3):
+        act(vw("eb", b, 528, 4), vw("dep", 0, 132), ACT.Copy, scale=0.0)
+    for b in (2, 3):
+        act(vw("cone", b, 648, 4), vw("dep", 0, 162), ACT.Copy, scale=0.0)
+        act(vw("rich", b, 512, 4), vw("dep", 0, 128), ACT.Copy, scale=0.0)
+    act(NK0, K7, scale=-1.0)
+    act(NK1, PEN, scale=-1.0, bias=NK0)
+    fill(vw("ts0", 0, 576), 0.0)
+    fill(vw("ts2", 0, 576), 0.0)
+    fill(vw("src1", 0, 16), 0.0)
+    iota(vw("li", 0, 10), [[16, 10]], 0)
+    cp(vw("lu", 0, 8), vw("li", 0, 8))
+    ts(vw("lf", 0, 9), vw("li", 0, 9), R, A.add)
+    tt(vw("lf", 30, 39), vw("lf", 0, 9), vw("li", 0, 9), A.add)
+    ts(vw("lu", 10, 19), vw("lf", 30, 39), R8, A.add)
+    ts(vw("li", 20, 29), vw("lf", 0, 9), 1.0 / 18, A.mult, -0.472, A.add)
+    ts(vw("lf", 10, 19), vw("li", 20, 29), -143.0 / 8, A.mult)
+    tt(vw("lf", 20, 29), vw("lf", 10, 19), vw("lf", 0, 9), A.add)
+    ts(vw("lu", 20, 29), vw("lf", 20, 29), 8.0, A.mult)
+    LU, LTOP, LDM = vw("lu", 0, 8), vw("lu", 10, 19), vw("lu", 20, 29)
+    iota(vw("icp", 0, 180), [[-1, 20], [0, 9]], 17)
+    for b in range(2):
+        a0, a1 = vw("ab", 324 * b, 324 * b + 162), vw("ab", 324 * b + 162, 324 * b + 324)
+        act(a0, vw("icp", 18 * b, 18 * b + 162), ACT.Abs, scale=-1.0, bias=C3)
+        act(a1, vw("dep", 0, 162), bias=(NK0, NK1)[b])
+        tt(vw("cone", b, 648, 4), a0, a1, A.is_le)
+    quant("cone", vw("cone", 0, 648))
+    iota(vw("bi", 0, 162), [[-4, 18], [72, 9]], 68)
+    iota(vw("bi", 162, 198), [[8, 2], [0, 18]], -76)
+    act(vw("bc", 0, 198), vw("bi", 0, 198), scale=1.0 / 2048)
+    ev = vw("eb", 3, 515, 4)
+    op("g", 460 * CYC, lambda q: q.affine_select(ap(ev), T.c64[:], [[-1, 128]], A.is_equal, 0.0, 0, 1), [vw("c64", 0, 128)], [ev])
+    for b in range(4):
+        quant("e", vw("eb", 3 - b, 515 - b), 128 * b)
+
+    def const(al, be, ga, deep=True):
+        v = new("ci")
+        iota(v, [[al, 18], [be, 2]], ga)
+        if not deep:
+            return v
+        out = vw("cc", v[1], v[2])
+        act(out, v, bias=I0)
+        return out
+
+    quant("u", vw("ub", 0, 512))
+    pick("up", "u", 128, LU)
+
+    def cuts(q):
+        for b in range(2):
+            mm(4 + b, q, 16 * b, "up", 0, 128)
+        for b in range(2):
+            ts(vw("rich", b, 512, 4), vw("ps", 512 * (4 + b), 512 * (4 + b) + 128), 0.0, A.is_gt, 0.5, A.subtract)
+        quant("rich", vw("rich", 0, 512))
+        mm(4, "rich", 0, "cone", 0, 162)
+        m, f, a = new("wf", 162), new("wf", 18), new("wf", 18)
+        scan(m, vw("ps", 2048, 2048 + 162), vw("bc", 0, 162), 8.0, A.max, A.min)
+        scan(f, vw("bc", 162, 180), step(m, 8, 9), 0.0, A.add, A.max)
+        scan(a, vw("bc", 180, 198), vw("wf", f[2] - 1, f[1] - 1, -1), 0.0, A.add, A.max)
+        return a
+
+    def slot_list(a, o):
+        for h, k in enumerate((KH0, KH1)):
+            ts(vw(o, h, 36, 2), a, 2048.0, A.mult, k, A.add)
+
+    def unlist(o, ex=EX):
+        out = new("wi")
+        ts(out, vw(o, 0, 36), 1.0 / 72, A.mult, ex, A.add)
+        return out
+
+    def add(a, b, o=A.add):
+        out = new("wf")
+        tt(out, a, b, o)
+        return out
+
+    def sub(a, b):
+        return add(a, b, A.subtract)
+
+    def mul(a, b):
+        return add(a, b, A.mult)
+
+    def to_off(col, base, dst=None, h0=0):
+        if dst is None:
+            out = new("off")
+            ts(out, col, 4.0, A.mult, base, A.add)
+            return out
+        for h in range(2):
+            ts(step(dst, h0 + h, 4), step(col, h, 2), 4.0, A.mult, base, A.add)
+        return dst
+
+    def step_of(s, v, at=0.0):
+        out = new("wf")
+        ts(out, s, at, A.is_ge, v, A.mult)
+        return out
+
+    VS = "vs"
+    SETA = (0, 1, 2, 3)
+    BK = (SETA, (6, 7, 7, 6))
+    C1, CS, CSE, CT, CD, CG = const(16, 8, -4), const(0, 8, -12), const(0, 4, -8), const(8, 8, -4), const(-8, 4, 137), const(-8, 0, 272, False)
+
+    quant("x0", vw("xb", 0, 1152))
+    pick("t0", "x0", 288, LTOP)
+    send(0, [(vw("q_t0", 0, 144), vw("q_l0", 0, 144))])
+    send(0, [(vw("s_t0", 0, 144), vw("s_l0", 0, 144))])
+    a0 = cuts("t0")
+    slot_list(a0, "o0")
+    send(0, [(vw("o0", 0, 36), vw("lo0", 0, 36))])
+    unpack("x0", 288, "src0", 0, SETA, O["e_t0"])
+    h0 = unlist("o0")
+    top0 = add(h0, C1)
+    gather2("x1t", vw("src0", 0, 1152), "off", VS, to_off(top0, TT)[1])
+    quant("x1t", vw("x1t", 0, 576))
+    a1 = cuts("x1t")
+    h1 = vw("a1", 0, 36)
+    for h in range(2):
+        ts(step(h1, h, 2), a1, 2048.0 / 72, A.mult, 4.0 - 4 * h - 0.472, A.add)
+    fl = new("wf")
+    ts(fl, h1, -5.0, A.add, I0, A.is_ge)
+    quant("f0", vw("src0", 0, 1152))
+    unpack("f0", 288, "src1", 16, BK[O["b_f0"]], O["e_f0"])
+    pick("d0", "l0", 144, LDM)
+    unpack("d0", 144, "ts0", 576, SETA, O["e_ts0"])
+    gather2("b0", vw("ts0", 0, 1152), "lo0", VS)
+    quant("b0", vw("b0", 0, 576))
+    g0 = unlist("lo0")
+    unpack("b0", 144, "h0", 0, SETA, "vvss", True)
+    quant("h0", vw("h0", 0, 576))
+    unpack("h0", 144, "src1", 16 + 1152, SETA, "vvss")
+
+    sg = add(h0, h1)
+    ob1 = to_off(mul(sub(sg, const(-16, -4, 5)), fl), TT)
+    gather2("b1", vw("src1", 0, 16 + 1152), "off", O["e_b1"], ob1[1])
+    s16 = add(sg, const(0, 12, -24))
+    se = add(s16, const(0, -4, 4, False))
+    own = add(h1, const(-16, 8, -19))
+    uu = add(s16, add(h1, const(0, 8, -3)))
+    dl = add(uu, mul(step_of(s16, 1.0), CG))
+    ot = to_off(sub(mul(add(se, g0, A.is_lt), dl), own), TT)
+    gather2("x2t", vw("src1", 16, 16 + 1728), "off", VS, ot[1])
+    u16 = new("wf")
+    ts(u16, uu, 16.0, A.add)
+    dl = add(u16, mul(step_of(s16, 1.0, -8.0), CG))
+    colp = sub(mul(add(se, unlist("lo0", EX8), A.is_lt), dl), own)
+    k16 = add(h1, CS)
+    mk = step_of(k16, 1.0)
+    evp = sub(h0, const(-16, 0, -11))
+    base = add(colp, mul(mk, sub(evp, colp)))
+    de = mul(mk, sub(add(k16, const(8, 0, 440, False)), evp))
+    k16e = add(h1, CSE)
+    quant("b1", vw("b1", 0, 576))
+    send(1, [(vw("q_b1", 0, 144), vw("q_l1", 0, 144))])
+    send(1, [(vw("s_b1", 0, 144), vw("s_l1", 0, 144)), (h1, vw("la1", 0, 36))])
+    quant("x2t", vw("x2t", 0, 576))
+
+    send(2, [(vw("q_x2t", 0, 144), vw("q_l2", 0, 144))])
+    send(2, [(vw("s_x2t", 0, 144), vw("s_l2", 0, 144))])
+    a2 = cuts("x2t")
+    slot_list(a2, "o2")
+    send(2, [(vw("o2", 0, 36), vw("lo2", 0, 36))])
+    unpack("l1", 144, "src1", 16 + 1728, BK[O["b_h1"]], O["e_h1"], True)
+    unpack("x2t", 144, "src2", 0, BK[O["b_t2t"]], O["e_t2t"])
+    ob = to_off(add(base, mul(add(k16e, vw("la1", 0, 36), A.is_lt), de)), TM32)
+    gather2("x2b", vw("src1", 16, 16 + 2304), "off", O["e_x2b"], ob[1])
+    quant("x2b", vw("x2b", 0, 576))
+    pick("d2", "l2", 144, LDM)
+    unpack("d2", 144, "ts2", 576, BK[O["b_ts2"]], O["e_ts2"])
+    unpack("x2b", 144, "src2", 576, BK[O["b_t2b"]], O["e_t2b"])
+    dma("y", T.vb[:], T.v[:], [vw(O["vat"], 0, 36)], [vw("vb", 0, 512)], 131072)
+    quant("v", vw("vb", 0, 512))
+    h2 = unlist("o2")
+    cp(vw("oaf", 0, 18), step(h2, 1, 2))
+    dma("y", T.oa[:], T.oaf[0:128:16, :], [vw("oaf", 0, 18)], [], 0)
+    top2 = add(add(h2, CT), step_of(add(h2, CS), 136.0))
+    o3 = new("off", 72)
+    to_off(top2, TT, o3, 0)
+    se2, d2 = add(h2, CSE), add(top2, CD)
+    gather2("b2", vw("ts2", 0, 1152), "lo2", VS)
+    quant("b2", vw("b2", 0, 576))
+    unpack("b2", 144, "src2", 1152, SETA, "vvss", True)
+    to_off(sub(mul(add(se2, unlist("lo2"), A.is_lt), d2), CD), T576, o3, 2)
+
+    for i, e in enumerate(VS):
+        gather(e, vw("x3", 576 * i, 576 * i + 576), vw("src2", 0, 1728), vw("off", o3[1] + 36 * i, o3[1] + 36 * i + 36))
+    for i in range(2):
+        quant("x3", vw("x3", 576 * i, 576 * i + 576), 144 * i)
+        mm(4 + i, "v", 0, "x3", 144 * i, 144)
+    dma("y", T.oc[:], T.q_x3[:].bitcast(dt.uint8), [vw("q_x3", 0, 288)], [], 150000)
+    for k in range(4):
+        dma("y" if k < 2 else "s", T.osc[4 * k:4 * k + 4, :], T.s_x3[32 * k:32 * k + 4, :], [vw("s_x3", 0, 288)], [], 0)
+    act(vw("yb", 0, 144), vw("ps", 2048, 2048 + 144), ACT.Copy)
+    cp(vw("yb", 144, 288), vw("ps", 2560, 2560 + 144))
+    dma("s", T.y[:], T.yb[:], [vw("yb", 0, 288)], [], 150000)
+    return ops
+
+
+def depend(ops):
+    last = {}
+    for o in ops:
+        deps = set()
+        for v, w in [(v, False) for v in o["r"]] + [(v, True) for v in o["w"]]:
+            bank = v[0] == "ps"
+            key = (v[0], v[1] // 512) if bank else v[0]
+            cs = None if bank else frozenset(cols(v))
+            for (j, cj, wj) in last.get(key, ()):
+                if j == o["id"]:
+                    continue
+                if bank:
+                    if ops[j]["eng"] != o["eng"] or w or wj:
+                        deps.add(j)
+                elif (w or wj) and not cs.isdisjoint(cj):
+                    deps.add(j)
+            last.setdefault(key, []).append((o["id"], cs, w))
+        o["deps"] = deps
+
+
+def rank_program(g, core, T, topo):
+    rank = T.rank_of(core)
+    if rank is None:
+        return
+    ops = plan(T, topo, core, rank)
+    depend(ops)
+    seq = [ops[i] for i in ORDER]
+    queue = {"v": g.vector, "s": g.scalar, "t": g.tensor, "g": g, "y": g.sync}
+    known, count = {e: {} for e in queue}, {e: 0 for e in queue}
+    for i, o in enumerate(seq):
+        o["place"] = i
+        if o["kind"] == "c":
+            count[o["eng"]] += 1
+            o["src"], o["at"] = o["eng"], count[o["eng"]]
+        else:
+            o["src"], o["at"] = ("x", o["id"]), 1
+        kn = known[o["eng"]]
+        need = {}
+        for j in o["deps"]:
+            d = ops[j]
+            if o["acc"] and d["eng"] == "t":
+                continue
+            if kn.get(d["src"], 0) < d["at"] and need.get(d["src"], {"at": 0})["at"] < d["at"]:
+                need[d["src"]] = d
+        waits = []
+        for d in sorted(need.values(), key=lambda d: -d["place"]):
+            if kn.get(d["src"], 0) < d["at"]:
+                waits.append(d)
+                d["inc"] = True
+                kn[d["src"]] = d["at"]
+                if d["kind"] != "r":
+                    for s, a in d["knew"].items():
+                        kn[s] = max(kn.get(s, 0), a)
+        o["waits"], o["knew"] = waits[::-1], dict(kn)
+    total, nd, nr, sent = {e: 0 for e in queue}, 0, 0, 0
+    for o in ops:
+        if o["kind"] == "r":
+            o["sem"], o["val"] = T.sem["ar%d" % nr], o["n"]
+            nr += 1
+        elif o["kind"] == "d":
+            o["sem"], o["val"] = T.sem["dm%d" % nd], 16
+            nd += 1
+    for o in seq:
+        q = queue[o["eng"]]
+        for d in o["waits"]:
+            q.wait_ge(d["sem"], d["val"])
+        if o["kind"] == "r":
+            o["fn"](q, o["sem"], T.sem.sent)
+            sent += o["n"]
+        elif o["kind"] == "d":
+            o["fn"](q).then_inc(o["sem"], 16)
+        elif o.get("inc"):
+            total[o["eng"]] += 1
+            o["sem"], o["val"] = T.sem["c" + o["eng"]], total[o["eng"]]
+            o["fn"](q).then_inc(o["sem"], 1)
+        else:
+            o["fn"](q)
+    g.wait_ge(T.sem.sent, sent)
+    for o in seq:
+        if o["kind"] == "d" and not o.get("inc"):
+            queue[o["eng"]].wait_ge(o["sem"], 16)

@@ -27,7 +27,7 @@ WIDE = {BF: 2, F32: 4, I32: 4, U16: 2, FP: 4, U8: 1}
 COST = {"cyc": 0.001, "gather": 1.56, "wake": 0.08, "pe": 0.00063, "call": 0.5, "far": 1.0, "row": 0.05, "byte": 0.00007, "first": 1.5}
 OPT = {"e_t0": "ssss", "e_f0": "ssss", "e_ts0": "vvss", "e_b1": "vs", "e_t2t": "ssss", "e_h1": "ssss", "e_x2b": "vs",
        "e_ts2": "vvss", "e_t2b": "ssss", "b_t2t": 1, "b_t2b": 1, "b_f0": 0, "b_h1": 0, "b_ts2": 0, "vat": "o2"}
-ORDER = [0, 4, 32, 1, 2, 3, 7, 9, 6, 5, 8, 10, 34, 43, 21, 20, 11, 35, 36, 12, 29, 47, 30, 44, 48, 45, 23, 24, 17, 22, 161, 54, 173, 168, 51, 62, 52, 37, 31, 38, 49, 46, 55, 56, 73, 74, 59, 76, 13, 162, 16, 14, 28, 26, 27, 174, 25, 75, 15, 61, 60, 50, 94, 90, 78, 77, 79, 80, 95, 91, 63, 53, 81, 82, 57, 58, 83, 92, 96, 84, 93, 19, 97, 33, 85, 39, 86, 88, 87, 40, 98, 99, 100, 101, 102, 103, 116, 104, 105, 199, 171, 70, 89, 68, 205, 66, 72, 64, 176, 106, 119, 117, 107, 108, 41, 109, 169, 200, 120, 118, 123, 121, 201, 42, 110, 111, 112, 114, 113, 125, 160, 115, 163, 124, 177, 122, 71, 18, 126, 178, 164, 170, 165, 129, 133, 127, 131, 175, 166, 167, 134, 130, 128, 132, 136, 65, 210, 135, 172, 212, 211, 137, 139, 142, 143, 145, 148, 146, 140, 149, 180, 193, 179, 138, 181, 190, 182, 183, 197, 147, 141, 184, 144, 150, 151, 156, 154, 155, 158, 152, 159, 185, 191, 194, 157, 186, 189, 153, 192, 187, 188, 198, 213, 195, 206, 217, 196, 216, 219, 240, 242, 218, 202, 241, 67, 214, 215, 220, 246, 221, 203, 209, 207, 204, 222, 208, 223, 248, 243, 247, 228, 234, 229, 237, 238, 235, 231, 224, 249, 226, 225, 227, 250, 275, 232, 244, 251, 276, 230, 239, 236, 233, 69, 253, 273, 277, 245, 252, 279, 254, 255, 256, 267, 265, 266, 268, 257, 263, 261, 259, 278, 284, 280, 281, 258, 269, 271, 264, 260, 262, 301, 285, 286, 287, 288, 298, 289, 299, 290, 292, 293, 295, 296, 270, 272, 294, 300, 302, 282, 303, 274, 304, 283, 305, 291, 306, 297, 307, 308, 309, 311, 310, 312, 313, 317, 318, 316, 319, 315, 314, 320]
+ORDER = [0, 4, 1, 2, 3, 33, 20, 42, 30, 12, 10, 7, 8, 6, 5, 19, 9, 31, 11, 34, 35, 53, 61, 51, 50, 22, 23, 21, 13, 28, 43, 17, 44, 15, 29, 14, 63, 36, 56, 37, 55, 57, 45, 54, 74, 58, 27, 18, 46, 64, 26, 52, 62, 47, 24, 16, 25, 76, 75, 93, 91, 95, 97, 60, 59, 38, 48, 39, 79, 80, 81, 82, 49, 94, 92, 96, 98, 83, 118, 84, 125, 121, 119, 123, 180, 65, 69, 174, 71, 170, 78, 77, 177, 73, 204, 162, 67, 210, 40, 85, 86, 87, 41, 100, 88, 89, 102, 101, 126, 171, 178, 181, 68, 70, 205, 104, 163, 66, 72, 124, 128, 120, 122, 99, 103, 172, 105, 206, 90, 107, 106, 32, 173, 182, 164, 109, 108, 175, 110, 127, 111, 112, 113, 133, 131, 129, 135, 134, 132, 136, 114, 130, 140, 116, 115, 137, 138, 165, 117, 183, 185, 166, 139, 167, 147, 148, 150, 141, 151, 144, 142, 145, 176, 184, 168, 149, 169, 152, 146, 215, 186, 143, 217, 216, 187, 188, 153, 195, 179, 189, 190, 154, 156, 158, 160, 157, 161, 155, 159, 191, 202, 196, 192, 193, 218, 219, 222, 221, 245, 247, 248, 246, 194, 197, 214, 211, 224, 223, 199, 212, 225, 203, 220, 226, 233, 236, 242, 239, 251, 249, 243, 237, 240, 234, 198, 200, 213, 227, 201, 228, 207, 229, 208, 253, 230, 231, 209, 254, 232, 244, 241, 235, 250, 252, 238, 260, 280, 255, 261, 256, 258, 283, 284, 281, 257, 268, 266, 278, 282, 262, 264, 269, 289, 285, 267, 265, 263, 259, 286, 291, 306, 292, 270, 272, 271, 273, 276, 290, 293, 307, 274, 297, 300, 294, 295, 301, 298, 303, 304, 288, 308, 309, 275, 277, 299, 305, 296, 311, 302, 310, 287, 279, 312, 313, 316, 314, 317, 315, 318, 324, 320, 319, 323, 322, 321, 325]
 
 
 def vw(name, a, b, step=1):
@@ -174,7 +174,7 @@ def plan(T, topo, core, rank, C=COST, O=OPT):
     dma("y", T.q_w[:].bitcast(dt.uint8), T.wc[:], [], [vw("q_w", 0, 512)], 262144)
     dma("y", T.s_w[:], T.ws[:], [], [vw("s_w", 0, 512)], 65536)
 
-    P, R, R8, TT, I0, K7, C3, PEN, KH0, KH1, EX, EX8, T576, TM32, KB, NK0, NK1 = [vw("pc", i, i + 1) for i in range(17)]
+    P, R, R8, TT, I0, K7, C3, PEN, KH0, KH1, EX, T576, TM32, KB, NK0, NK1, KX0, KX1 = [vw("pc", i, i + 1) for i in range(18)]
     p = vw("pi", 0, 1)
     iota(p, [[0, 1]], 0, 1)
     ts(vw("pi", 1, 2), p, 15, A.bitwise_and)
@@ -190,7 +190,6 @@ def plan(T, topo, core, rank, C=COST, O=OPT):
     act(KH1, KB, bias=216.0)
     act(EX, KB, scale=-1.0 / 72, bias=-3.472)
     act(T576, TT, bias=576.0)
-    act(EX8, KB, scale=-1.0 / 72, bias=-11.472)
     act(TM32, TT, bias=-32.0)
     fill(vw("c64", 0, 128), 64.0)
     iota(vw("dep", 0, 162), [[0, 18], [1, 9]], -1)
@@ -258,9 +257,9 @@ def plan(T, topo, core, rank, C=COST, O=OPT):
         for h, k in enumerate((KH0, KH1)):
             ts(vw(o, h, 36, 2), a, 2048.0, A.mult, k, A.add)
 
-    def unlist(o, ex=EX):
+    def unlist(o):
         out = new("wi")
-        ts(out, vw(o, 0, 36), 1.0 / 72, A.mult, ex, A.add)
+        ts(out, vw(o, 0, 36), 1.0 / 72, A.mult, EX, A.add)
         return out
 
     def add(a, b, o=A.add):
@@ -283,15 +282,20 @@ def plan(T, topo, core, rank, C=COST, O=OPT):
             ts(step(dst, h0 + h, 4), step(col, h, 2), 4.0, A.mult, base, A.add)
         return dst
 
-    def step_of(s, v, at=0.0):
+    def step_of(s, v):
         out = new("wf")
-        ts(out, s, at, A.is_ge, v, A.mult)
+        ts(out, s, 0.0, A.is_ge, v, A.mult)
         return out
 
     VS = "vs"
     SETA = (0, 1, 2, 3)
     BK = (SETA, (6, 7, 7, 6))
-    C1, CS, CSE, CT, CD, CG = const(16, 8, -4), const(0, 8, -12), const(0, 4, -8), const(8, 8, -4), const(-8, 4, 137), const(-8, 0, 272, False)
+    iota(vw("ci", 0, 18), [[1148, 18]], 0)
+    act(vw("cc", 0, 18), vw("ci", 0, 18), scale=1.0 / 2048)
+    new("ci")
+    act(KX0, I0, scale=4.0, bias=TT)
+    act(KX1, KX0, bias=16.0)
+    CS, CSE, CT, CD, CG = const(0, 8, -12), const(0, 4, -8), const(8, 8, -4), const(-8, 4, 137), const(-8, 0, 272, False)
 
     quant("x0", vw("xb", 0, 1152))
     pick("t0", "x0", 288, LTOP)
@@ -302,8 +306,11 @@ def plan(T, topo, core, rank, C=COST, O=OPT):
     send(0, [(vw("o0", 0, 36), vw("lo0", 0, 36))])
     unpack("x0", 288, "src0", 0, SETA, O["e_t0"])
     h0 = unlist("o0")
-    top0 = add(h0, C1)
-    gather2("x1t", vw("src0", 0, 1152), "off", VS, to_off(top0, TT)[1])
+    y0, o1 = new("wf", 18), new("off")
+    tt(y0, a0, vw("cc", 0, 18), A.add)
+    for h, k in enumerate((KX0, KX1)):
+        ts(step(o1, h, 2), y0, 2048.0 / 18, A.mult, k, A.add)
+    gather2("x1t", vw("src0", 0, 1152), "off", VS, o1[1])
     quant("x1t", vw("x1t", 0, 576))
     a1 = cuts("x1t")
     h1 = vw("a1", 0, 36)
@@ -322,20 +329,21 @@ def plan(T, topo, core, rank, C=COST, O=OPT):
     quant("h0", vw("h0", 0, 576))
     unpack("h0", 144, "src1", 16 + 1152, SETA, "vvss")
 
-    sg = add(h0, h1)
-    ob1 = to_off(mul(sub(sg, const(-16, -4, 5)), fl), TT)
+    ob1 = to_off(mul(add(h1, sub(h0, const(-16, -4, 5))), fl), TT)
     gather2("b1", vw("src1", 0, 16 + 1152), "off", O["e_b1"], ob1[1])
-    s16 = add(sg, const(0, 12, -24))
-    se = add(s16, const(0, -4, 4, False))
+    pk, npk = add(h0, const(0, 12, -24)), new("wf")
+    ts(npk, pk, -1.0, A.mult)
+    lim = add(g0, sub(npk, const(0, -4, 4, False)))
     own = add(h1, const(-16, 8, -19))
-    uu = add(s16, add(h1, const(0, 8, -3)))
-    dl = add(uu, mul(step_of(s16, 1.0), CG))
-    ot = to_off(sub(mul(add(se, g0, A.is_lt), dl), own), TT)
+    uu = add(h1, add(h1, add(pk, const(0, 8, -3))))
+    dl = add(uu, mul(add(h1, npk, A.is_ge), CG))
+    ot = to_off(sub(mul(add(h1, lim, A.is_lt), dl), own), TT)
     gather2("x2t", vw("src1", 16, 16 + 1728), "off", VS, ot[1])
-    u16 = new("wf")
+    u16, h8 = new("wf"), new("wf")
     ts(u16, uu, 16.0, A.add)
-    dl = add(u16, mul(step_of(s16, 1.0, -8.0), CG))
-    colp = sub(mul(add(se, unlist("lo0", EX8), A.is_lt), dl), own)
+    ts(h8, h1, 8.0, A.add)
+    dl = add(u16, mul(add(h8, npk, A.is_ge), CG))
+    colp = sub(mul(add(h8, lim, A.is_lt), dl), own)
     k16 = add(h1, CS)
     mk = step_of(k16, 1.0)
     evp = sub(h0, const(-16, 0, -11))

@@ -13,7 +13,7 @@ for _n, _w in (("u", 128), ("up", 128), ("v", 128), ("w", 512), ("e", 512), ("co
                ("l1", 144), ("x2t", 144), ("l2", 144), ("d2", 144), ("x2b", 144), ("b2", 144), ("x3", 288)):
     SCRATCH["q_" + _n] = ("sbuf", [128, _w], FP)
     SCRATCH["s_" + _n] = ("sbuf", [128, _w], U8)
-for _n, _w, _d in (("pi", 8, I32), ("pc", 24, F32), ("cc", 576, F32), ("ci", 576, F32), ("bi", 198, F32), ("bc", 198, F32),
+for _n, _w, _d in (("pi", 8, I32), ("pc", 24, F32), ("cc", 576, F32), ("ci", 576, F32), ("bi", 396, F32), ("bc", 396, F32),
                    ("li", 64, I32), ("lf", 64, F32), ("lu", 40, U16), ("wf", 4000, F32), ("wi", 256, I32), ("off", 320, U16),
                    ("o0", 36, U16), ("o2", 36, U16), ("lo0", 36, U16), ("lo2", 36, U16), ("a1", 36, I32),
                    ("la1", 36, I32), ("oaf", 18, F32), ("yb", 288, F32)):
@@ -26,8 +26,8 @@ ACT = ActivationFunctionType
 WIDE = {BF: 2, F32: 4, I32: 4, U16: 2, FP: 4, U8: 1}
 COST = {"cyc": 0.001, "gather": 1.56, "wake": 0.08, "pe": 0.00063, "call": 0.5, "far": 1.0, "row": 0.05, "byte": 0.00007, "first": 1.5}
 OPT = {"e_t0": "ssss", "e_f0": "ssss", "e_ts0": "vvss", "e_b1": "vs", "e_t2t": "ssss", "e_h1": "ssss", "e_x2b": "vs",
-       "e_ts2": "vvss", "e_t2b": "ssss", "b_t2t": 1, "b_t2b": 1, "b_f0": 0, "b_h1": 0, "b_ts2": 0, "vat": "o2"}
-ORDER = [0, 4, 1, 2, 3, 33, 20, 42, 30, 12, 10, 7, 8, 6, 5, 19, 9, 31, 11, 34, 35, 53, 61, 51, 50, 22, 23, 21, 13, 28, 43, 17, 44, 15, 29, 14, 63, 36, 56, 37, 55, 57, 45, 54, 74, 58, 27, 18, 46, 64, 26, 52, 62, 47, 24, 16, 25, 76, 75, 93, 91, 95, 97, 60, 59, 38, 48, 39, 79, 80, 81, 82, 49, 94, 92, 96, 98, 83, 118, 84, 125, 121, 119, 123, 180, 65, 69, 174, 71, 170, 78, 77, 177, 73, 204, 162, 67, 210, 40, 85, 86, 87, 41, 100, 88, 89, 102, 101, 126, 171, 178, 181, 68, 70, 205, 104, 163, 66, 72, 124, 128, 120, 122, 99, 103, 172, 105, 206, 90, 107, 106, 32, 173, 182, 164, 109, 108, 175, 110, 127, 111, 112, 113, 133, 131, 129, 135, 134, 132, 136, 114, 130, 140, 116, 115, 137, 138, 165, 117, 183, 185, 166, 139, 167, 147, 148, 150, 141, 151, 144, 142, 145, 176, 184, 168, 149, 169, 152, 146, 215, 186, 143, 217, 216, 187, 188, 153, 195, 179, 189, 190, 154, 156, 158, 160, 157, 161, 155, 159, 191, 202, 196, 192, 193, 218, 219, 222, 221, 245, 247, 248, 246, 194, 197, 214, 211, 224, 223, 199, 212, 225, 203, 220, 226, 233, 236, 242, 239, 251, 249, 243, 237, 240, 234, 198, 200, 213, 227, 201, 228, 207, 229, 208, 253, 230, 231, 209, 254, 232, 244, 241, 235, 250, 252, 238, 260, 280, 255, 261, 256, 258, 283, 284, 281, 257, 268, 266, 278, 282, 262, 264, 269, 289, 285, 267, 265, 263, 259, 286, 291, 306, 292, 270, 272, 271, 273, 276, 290, 293, 307, 274, 297, 300, 294, 295, 301, 298, 303, 304, 288, 308, 309, 275, 277, 299, 305, 296, 311, 302, 310, 287, 279, 312, 313, 316, 314, 317, 315, 318, 324, 320, 319, 323, 322, 321, 325]
+       "e_ts2": "vvss", "e_t2b": "ssss", "b_t2t": 1, "b_t2b": 1, "b_f0": 1, "b_h1": 0, "b_ts2": 0, "vat": "o2"}
+ORDER = [0, 4, 20, 31, 40, 1, 2, 3, 29, 8, 9, 6, 5, 7, 10, 12, 11, 28, 33, 45, 30, 42, 19, 34, 32, 62, 26, 41, 23, 44, 178, 171, 68, 60, 51, 59, 49, 48, 43, 35, 46, 36, 73, 172, 13, 21, 24, 18, 25, 15, 14, 22, 75, 56, 74, 58, 27, 63, 61, 16, 50, 57, 78, 79, 76, 55, 53, 47, 80, 81, 37, 82, 52, 54, 97, 99, 83, 93, 95, 98, 100, 96, 94, 77, 181, 175, 207, 72, 163, 70, 66, 64, 213, 87, 84, 88, 38, 85, 89, 39, 86, 103, 102, 90, 91, 104, 105, 129, 71, 69, 92, 128, 106, 107, 101, 119, 108, 130, 132, 134, 173, 109, 136, 110, 131, 135, 164, 133, 137, 111, 174, 138, 122, 120, 112, 139, 123, 182, 208, 17, 67, 121, 113, 140, 114, 176, 141, 209, 115, 165, 179, 177, 124, 148, 149, 142, 143, 151, 145, 146, 152, 116, 117, 150, 126, 144, 166, 118, 65, 125, 147, 153, 127, 180, 186, 189, 184, 167, 183, 187, 185, 168, 154, 190, 188, 170, 169, 155, 157, 159, 161, 191, 156, 158, 160, 162, 192, 218, 195, 196, 198, 193, 205, 221, 220, 219, 199, 214, 194, 222, 224, 225, 248, 250, 215, 197, 226, 223, 227, 206, 251, 249, 217, 200, 228, 202, 216, 201, 203, 229, 254, 230, 204, 256, 231, 210, 232, 211, 257, 242, 236, 239, 240, 237, 243, 245, 246, 252, 234, 233, 212, 235, 263, 283, 258, 287, 259, 284, 286, 241, 238, 244, 255, 247, 264, 253, 261, 288, 260, 281, 285, 265, 267, 269, 271, 266, 268, 270, 272, 262, 289, 294, 295, 273, 275, 274, 309, 292, 293, 276, 296, 310, 291, 311, 290, 312, 279, 277, 278, 280, 297, 303, 300, 298, 306, 307, 301, 304, 282, 299, 314, 313, 305, 308, 302, 315, 316, 317, 319, 318, 320, 323, 321, 322, 324, 326, 325, 327, 328]
 
 
 def vw(name, a, b, step=1):
@@ -174,7 +174,7 @@ def plan(T, topo, core, rank, C=COST, O=OPT):
     dma("y", T.q_w[:].bitcast(dt.uint8), T.wc[:], [], [vw("q_w", 0, 512)], 262144)
     dma("y", T.s_w[:], T.ws[:], [], [vw("s_w", 0, 512)], 65536)
 
-    P, R, R8, TT, I0, K7, C3, PEN, KH0, KH1, EX, T576, TM32, KB, NK0, NK1, KX0, KX1 = [vw("pc", i, i + 1) for i in range(18)]
+    P, R, R8, TT, I0, K7, C3, PEN, KH0, KH1, EX, T576, TM32, KB, KX0, KX1 = [vw("pc", i, i + 1) for i in range(16)]
     p = vw("pi", 0, 1)
     iota(p, [[0, 1]], 0, 1)
     ts(vw("pi", 1, 2), p, 15, A.bitwise_and)
@@ -198,8 +198,6 @@ def plan(T, topo, core, rank, C=COST, O=OPT):
     for b in (2, 3):
         act(vw("cone", b, 648, 4), vw("dep", 0, 162), ACT.Copy, scale=0.0)
         act(vw("rich", b, 512, 4), vw("dep", 0, 128), ACT.Copy, scale=0.0)
-    act(NK0, K7, scale=-1.0)
-    act(NK1, PEN, scale=-1.0, bias=NK0)
     fill(vw("ts0", 0, 576), 0.0)
     fill(vw("ts2", 0, 576), 0.0)
     fill(vw("src1", 0, 16), 0.0)
@@ -217,7 +215,10 @@ def plan(T, topo, core, rank, C=COST, O=OPT):
     for b in range(2):
         a0, a1 = vw("ab", 324 * b, 324 * b + 162), vw("ab", 324 * b + 162, 324 * b + 324)
         act(a0, vw("icp", 18 * b, 18 * b + 162), ACT.Abs, scale=-1.0, bias=C3)
-        act(a1, vw("dep", 0, 162), bias=(NK0, NK1)[b])
+        if b:
+            ts(a1, vw("dep", 0, 162), K7, A.subtract, PEN, A.subtract)
+        else:
+            ts(a1, vw("dep", 0, 162), K7, A.subtract)
         tt(vw("cone", b, 648, 4), a0, a1, A.is_le)
     quant("cone", vw("cone", 0, 648))
     iota(vw("bi", 0, 162), [[-4, 18], [72, 9]], 68)
@@ -247,10 +248,13 @@ def plan(T, topo, core, rank, C=COST, O=OPT):
             ts(vw("rich", b, 512, 4), vw("ps", 512 * (4 + b), 512 * (4 + b) + 128), 0.0, A.is_gt, 0.5, A.subtract)
         quant("rich", vw("rich", 0, 512))
         mm(4, "rich", 0, "cone", 0, 162)
+        return reach(0)
+
+    def reach(k):
         m, f, a = new("wf", 162), new("wf", 18), new("wf", 18)
-        scan(m, vw("ps", 2048, 2048 + 162), vw("bc", 0, 162), 8.0, A.max, A.min)
-        scan(f, vw("bc", 162, 180), step(m, 8, 9), 0.0, A.add, A.max)
-        scan(a, vw("bc", 180, 198), vw("wf", f[2] - 1, f[1] - 1, -1), 0.0, A.add, A.max)
+        scan(m, vw("ps", 2048, 2048 + 162), vw("bc", k, k + 162), 8.0, A.max, A.min)
+        scan(f, vw("bc", k + 162, k + 180), step(m, 8, 9), -1.0, A.add, A.max)
+        scan(a, vw("bc", k + 180, k + 198), vw("wf", f[2] - 1, f[1] - 1, -1), -1.0, A.add, A.max)
         return a
 
     def slot_list(a, o):
@@ -290,8 +294,9 @@ def plan(T, topo, core, rank, C=COST, O=OPT):
     VS = "vs"
     SETA = (0, 1, 2, 3)
     BK = (SETA, (6, 7, 7, 6))
-    iota(vw("ci", 0, 18), [[1148, 18]], 0)
-    act(vw("cc", 0, 18), vw("ci", 0, 18), scale=1.0 / 2048)
+    iota(vw("bi", 198, 360), [[-64, 18], [4, 9]], 1088)
+    iota(vw("bi", 360, 396), [[128, 2], [0, 18]], -68)
+    act(vw("bc", 198, 396), vw("bi", 198, 396), scale=1.0 / 4096)
     new("ci")
     act(KX0, I0, scale=4.0, bias=TT)
     act(KX1, KX0, bias=16.0)
@@ -302,14 +307,14 @@ def plan(T, topo, core, rank, C=COST, O=OPT):
     send(0, [(vw("q_t0", 0, 144), vw("q_l0", 0, 144))])
     send(0, [(vw("s_t0", 0, 144), vw("s_l0", 0, 144))])
     a0 = cuts("t0")
+    y0 = reach(198)
     slot_list(a0, "o0")
     send(0, [(vw("o0", 0, 36), vw("lo0", 0, 36))])
     unpack("x0", 288, "src0", 0, SETA, O["e_t0"])
     h0 = unlist("o0")
-    y0, o1 = new("wf", 18), new("off")
-    tt(y0, a0, vw("cc", 0, 18), A.add)
+    o1 = new("off")
     for h, k in enumerate((KX0, KX1)):
-        ts(step(o1, h, 2), y0, 2048.0 / 18, A.mult, k, A.add)
+        ts(step(o1, h, 2), y0, 4096.0, A.mult, k, A.add)
     gather2("x1t", vw("src0", 0, 1152), "off", VS, o1[1])
     quant("x1t", vw("x1t", 0, 576))
     a1 = cuts("x1t")
@@ -334,10 +339,12 @@ def plan(T, topo, core, rank, C=COST, O=OPT):
     pk, npk = add(h0, const(0, 12, -24)), new("wf")
     ts(npk, pk, -1.0, A.mult)
     lim = add(g0, sub(npk, const(0, -4, 4, False)))
-    own = add(h1, const(-16, 8, -19))
-    uu = add(h1, add(h1, add(pk, const(0, 8, -3))))
-    dl = add(uu, mul(add(h1, npk, A.is_ge), CG))
-    ot = to_off(sub(mul(add(h1, lim, A.is_lt), dl), own), TT)
+    n1 = add(h1, add(pk, const(16, 0, 16, False)))
+    w1 = add(h1, const(-24, 8, 253))
+    kept = add(mul(add(h1, lim, A.is_lt), n1), mul(add(h1, npk, A.is_ge), CG))
+    ot = to_off(sub(kept, mul(add(h1, lim, A.is_ge), w1)), TT)
+    own = sub(w1, CG)
+    uu = add(n1, own)
     gather2("x2t", vw("src1", 16, 16 + 1728), "off", VS, ot[1])
     u16, h8 = new("wf"), new("wf")
     ts(u16, uu, 16.0, A.add)

@@ -2,21 +2,20 @@ from concourse.bass import DstId, RemoteDMATransfer
 from concourse.mybir import dt, AluOpType, ActivationFunctionType
 
 BF, F32, I32, U16, FP, U8 = "bfloat16", "float32", "int32", "uint16", "float8_e4m3fn_x4", "uint8"
-SCRATCH = {"ps": ("psum", [128, 4096], F32)}
-for _n, _w in (("xb", 1152), ("ub", 512), ("vb", 512), ("src0", 1152), ("src1", 2320), ("src2", 1728), ("ts0", 1152),
-               ("ts2", 1152), ("x1t", 576), ("h0", 576), ("x2t", 576), ("x2b", 576), ("b0", 576), ("b1", 576),
-               ("b2", 576), ("x3", 1152), ("rich", 512), ("cone", 648), ("eb", 528), ("c64", 128),
-               ("icp", 180), ("dep", 162), ("ab", 648)):
+SCRATCH = {"ps": ("psum", [128, 4096], F32), "yb": ("sbuf", [128, 18, 16], F32)}
+for _n, _w in (("ub", 512), ("vb", 512), ("x0", 1152), ("x1", 576), ("x2", 1152), ("x3", 1152), ("src0", 1152), ("src1", 2320),
+               ("src2", 1728), ("win", 1152), ("win1", 592), ("b0", 576), ("b1", 576), ("b2", 576), ("h0", 576), ("rich", 512), ("cone0", 648),
+               ("cone1", 648), ("eb", 528), ("c64", 288), ("icp", 252), ("dep", 252), ("ab", 1008)):
     SCRATCH[_n] = ("sbuf", [128, _w], BF)
-for _n, _w in (("u", 128), ("up", 128), ("v", 128), ("w", 512), ("e", 512), ("cone", 162), ("rich", 128), ("x0", 288),
-               ("t0", 144), ("l0", 144), ("d0", 144), ("x1t", 144), ("h0", 144), ("b0", 144), ("b1", 144), ("f0", 288),
-               ("l1", 144), ("x2t", 144), ("l2", 144), ("d2", 144), ("x2b", 144), ("b2", 144), ("x3", 288)):
+for _n, _w in (("u", 128), ("up", 128), ("v", 128), ("w", 512), ("e", 512), ("cone0", 162), ("cone1", 162), ("rich", 128),
+               ("x0", 288), ("x1", 144), ("x2", 288), ("x3", 288), ("last", 288), ("d0", 144), ("d1", 144), ("d2", 144), ("l0", 144),
+               ("l1", 144), ("l2", 144), ("b0", 144), ("b1", 144), ("b2", 144), ("f0", 288), ("h0", 144)):
     SCRATCH["q_" + _n] = ("sbuf", [128, _w], FP)
     SCRATCH["s_" + _n] = ("sbuf", [128, _w], U8)
-for _n, _w, _d in (("pi", 8, I32), ("pc", 24, F32), ("cc", 576, F32), ("ci", 576, F32), ("bi", 396, F32), ("bc", 396, F32),
-                   ("li", 64, I32), ("lf", 64, F32), ("lu", 40, U16), ("wf", 4000, F32), ("wi", 256, I32), ("off", 320, U16),
-                   ("o0", 36, U16), ("o2", 36, U16), ("lo0", 36, U16), ("lo2", 36, U16), ("a1", 36, I32),
-                   ("la1", 36, I32), ("oaf", 18, F32), ("yb", 288, F32)):
+for _n, _w, _d in (("pi", 9, I32), ("pr", 15, I32), ("pc", 36, F32), ("bc", 792, F32), ("li", 50, I32), ("lu", 48, U16),
+                   ("wf", 3000, F32), ("p", 756, F32), ("m", 756, F32),
+                   ("off", 288, U16), ("o0", 36, U16), ("o1", 72, U16), ("o2", 36, U16), ("lo0", 36, U16), ("lo1", 72, U16),
+                   ("lo2", 36, U16), ("oaf", 18, F32)):
     SCRATCH[_n] = ("sbuf", [128, _w], _d)
 
 SEMAPHORES = ["cv", "cs", "ct", "cg", "sent"] + ["dm%d" % i for i in range(16)] + ["ar%d" % i for i in range(10)]
@@ -24,10 +23,23 @@ SEMAPHORES = ["cv", "cs", "ct", "cg", "sent"] + ["dm%d" % i for i in range(16)] 
 A = AluOpType
 ACT = ActivationFunctionType
 WIDE = {BF: 2, F32: 4, I32: 4, U16: 2, FP: 4, U8: 1}
-COST = {"cyc": 0.001, "gather": 1.56, "wake": 0.08, "pe": 0.00063, "call": 0.5, "far": 1.0, "row": 0.05, "byte": 0.00007, "first": 1.5}
-OPT = {"e_t0": "ssss", "e_f0": "ssss", "e_ts0": "vvss", "e_b1": "vs", "e_t2t": "ssss", "e_h1": "ssss", "e_x2b": "vs",
-       "e_ts2": "vvss", "e_t2b": "ssss", "b_t2t": 1, "b_t2b": 1, "b_f0": 1, "b_h1": 0, "b_ts2": 0, "vat": "o2"}
-ORDER = [0, 4, 20, 31, 40, 1, 2, 3, 29, 8, 9, 6, 5, 7, 10, 12, 11, 28, 33, 45, 30, 42, 19, 34, 32, 62, 26, 41, 23, 44, 178, 171, 68, 60, 51, 59, 49, 48, 43, 35, 46, 36, 73, 172, 13, 21, 24, 18, 25, 15, 14, 22, 75, 56, 74, 58, 27, 63, 61, 16, 50, 57, 78, 79, 76, 55, 53, 47, 80, 81, 37, 82, 52, 54, 97, 99, 83, 93, 95, 98, 100, 96, 94, 77, 181, 175, 207, 72, 163, 70, 66, 64, 213, 87, 84, 88, 38, 85, 89, 39, 86, 103, 102, 90, 91, 104, 105, 129, 71, 69, 92, 128, 106, 107, 101, 119, 108, 130, 132, 134, 173, 109, 136, 110, 131, 135, 164, 133, 137, 111, 174, 138, 122, 120, 112, 139, 123, 182, 208, 17, 67, 121, 113, 140, 114, 176, 141, 209, 115, 165, 179, 177, 124, 148, 149, 142, 143, 151, 145, 146, 152, 116, 117, 150, 126, 144, 166, 118, 65, 125, 147, 153, 127, 180, 186, 189, 184, 167, 183, 187, 185, 168, 154, 190, 188, 170, 169, 155, 157, 159, 161, 191, 156, 158, 160, 162, 192, 218, 195, 196, 198, 193, 205, 221, 220, 219, 199, 214, 194, 222, 224, 225, 248, 250, 215, 197, 226, 223, 227, 206, 251, 249, 217, 200, 228, 202, 216, 201, 203, 229, 254, 230, 204, 256, 231, 210, 232, 211, 257, 242, 236, 239, 240, 237, 243, 245, 246, 252, 234, 233, 212, 235, 263, 283, 258, 287, 259, 284, 286, 241, 238, 244, 255, 247, 264, 253, 261, 288, 260, 281, 285, 265, 267, 269, 271, 266, 268, 270, 272, 262, 289, 294, 295, 273, 275, 274, 309, 292, 293, 276, 296, 310, 291, 311, 290, 312, 279, 277, 278, 280, 297, 303, 300, 298, 306, 307, 301, 304, 282, 299, 314, 313, 305, 308, 302, 315, 316, 317, 319, 318, 320, 323, 321, 322, 324, 326, 325, 327, 328]
+COST = {"cyc": 0.00088, "gather": 1.56, "wake": 0.25, "pe": 0.00055, "call": 0.2, "far": 0.5, "row": 0.015, "byte": 0.00004,
+        "first": 0.8, "issue": 0.2, "pre": 0.45, "post": 0.3, "patience": 0.5, "pause": 0.2, "busy": 1.1, "slow": 1.2}
+OPT = {"t0": ("ssss", 0), "w0": ("ssvs", 6), "h0": ("svss", 0), "f0": ("ssss", 1), "dh0": ("sssv", 0), "t2t": ("ssss", 1),
+       "h1": ("ssss", 0), "w1": ("ssss", 0), "w2": ("svvs", 4), "t2b": ("ssvs", 4), "h2": ("svsv", 0),
+       "x1t": 18, "b0": 18, "b1": 10, "x2t": 18, "x2b": 18, "b2": 18, "x3t": 18, "x3b": 18, "y": "ss", "fill": "sgsggsggg",
+       "vat": "lo0", "out": "yyyss"}
+BANKS = ((0, 1, 2, 3), (6, 7, 6, 7), (0, 1, 0, 1), (2, 3, 2, 3), (4, 5, 6, 7), (0, 1, 6, 7), (2, 3, 4, 5), (6, 7, 0, 1))
+NB = len(BANKS)
+LATE = {"o1:0+": 0.3, "dh0*:1+": -0.5, "deep:0": 9.3, "q_e:384": 5.2}
+ROWS = ["pi li pc:28 bc icp dep eb:3 bc:198 tab0 s_l0 q_l0 lo0 tab3 tab6 q_l1 s_l1 min:1 pin:3 px2b:2 mx2b:1 mx2b tab4 rows up down mtop"
+        " mtop:1 mtop:3 lo1",
+        "c64 eb pr q_x0 q_u q_d0 rich0 q_cone0 q_rich0 mdeep0 mnat fdeep0 fnat adeep0 n0 o0 o0:1 ox1t ox1t:1 x1t:v q_f0 q_x1 b0:v"
+        " rich1 q_b0 q_rich1 mflat fflat n1:1 n1 q_h0 px2t mx2t:2 mx2t:3 runx2t o1 ox2t"
+        " x2t:v q_x2 q_d2 rich2 q_rich2 got1 b1:v min:2 mdeep2 runin q_b1 fdeep2 adeep2 runx2b o2 o2:1 ox2b runtop"
+        " x2b:v q_x2:144 b2:v q_b2 x3t:v x3b:v q_x3:144 q_last:160 q_last", "s_last yb:1 s_last:160",
+        "s_d0 s_up rich0:1 x1t:s w0:0 w0:3 b0:s rich1:1 f0:0 h0:0 f0:1 x2t:s w1:3 s_d2 rich2:1 b1:s t2t:0",
+        "score0 score0:1 w0*:3 f0*:0 f0*:1 h0*:2 h0*:3 h0*:1", "x0 ub q_w s_w"]
 
 
 def vw(name, a, b, step=1):
@@ -47,9 +59,22 @@ def plan(T, topo, core, rank, C=COST, O=OPT):
     def ap(v):
         return T[v[0]][:, v[1]:v[2]:v[3]] if v[3] != 1 else T[v[0]][:, v[1]:v[2]]
 
+    labels = []
+
+    def name_of(v, reads):
+        if v[0] == "ps":
+            return "%s:%d*%s:%d" % (reads[0][0][2:], reads[0][1], reads[2][0][2:], reads[2][1])
+        for buf, a, b, label in labels:
+            if buf == v[0] and a <= min(v[1], v[2] - v[3]) < b:
+                return "%s:%d" % (label, v[1] - a)
+        return "%s:%d" % v[:2]
+
     def op(eng, dur, fn, reads, writes, kind="c", lat=0.0, acc=False):
         ops.append({"eng": eng, "dur": dur, "fn": fn, "r": [v for v in reads if isinstance(v, tuple)], "w": list(writes),
-                    "kind": kind, "lat": lat, "acc": acc, "id": len(ops)})
+                    "kind": kind, "lat": lat, "acc": acc, "id": len(ops),
+                    "name": name_of(writes[0], reads) if writes else "out%d" % len(ops)})
+        while any(o["name"] == ops[-1]["name"] for o in ops[:-1]):
+            ops[-1]["name"] += "'"
         return ops[-1]
 
     def sc(x):
@@ -77,7 +102,8 @@ def plan(T, topo, core, rank, C=COST, O=OPT):
         return op("v", vdur(len(cols(out)), 0.5 if narrow(out) else 1.0), lambda q: q.memset(ap(out), val), [], [out])
 
     def scan(out, d0, d1, init, o0, o1):
-        return op("v", vdur(len(cols(out))), lambda q: q.tensor_tensor_scan(ap(out), ap(d0), ap(d1), init, o0, o1), [d0, d1], [out])
+        d = vdur(len(cols(out)), 0.5 if narrow(out, d0, d1) else 1.0)
+        return op("v", d, lambda q: q.tensor_tensor_scan(ap(out), ap(d0), ap(d1), init, o0, o1), [d0, d1], [out])
 
     def act(out, a, func=None, bias=0.0, scale=1.0):
         f = ACT.Identity if func is None else func
@@ -86,6 +112,11 @@ def plan(T, topo, core, rank, C=COST, O=OPT):
         else:
             fn = lambda q: q.activation(ap(out), ap(a), f, bias=sc(bias), scale=scale)
         return op("s", vdur(len(cols(out))), fn, [a, bias], [out])
+
+    def sfill(out, val, eng="s"):
+        if eng == "g":
+            return iota(out, [[0, len(cols(out))]], int(val))
+        return act(out, vw("c64", 0, len(cols(out))), ACT.Identity if val else ACT.Copy, val, 0.0)
 
     def iota(out, pat, base, cm=0):
         if SCRATCH[out[0]][2] != I32:
@@ -99,44 +130,50 @@ def plan(T, topo, core, rank, C=COST, O=OPT):
         qv, sv = vw("q_" + name, a, a + m), vw("s_" + name, a, a + m)
         return op("v", (15 + 1.06 * m) * CYC, lambda q: q.quantize_mx(ap(qv), ap(sv), ap(src)), [src], [qv, sv])
 
-    def mm(bank, lhs, la, rhs, ra, m, start=True, stop=True):
+    def mm(bank, lhs, la, rhs, ra, m):
         out = vw("ps", 512 * bank, 512 * bank + m)
-        lq, ls = vw("q_" + lhs, la, la + 128), vw("s_" + lhs, la, la + 128)
+        ls = [(vw("q_" + x, la, la + 128), vw("s_" + x, la, la + 128)) for x in lhs.split("+")]
         rq, rs = vw("q_" + rhs, ra, ra + m), vw("s_" + rhs, ra, ra + m)
-        return op("t", (m + 16) * C["pe"], lambda q: q.matmul_mx(ap(out), ap(lq), ap(ls), ap(rq), ap(rs), start, stop),
-                  [lq, ls, rq, rs], [out], acc=not start)
 
-    def gather(eng, out, win, offs):
-        d = (60 + len(cols(out)) * C["gather"]) * CYC
-        if eng == "v":
-            return op("v", d, lambda q: q.tensor_copy(ap(out), ap(win).indirect(ap(offs))), [win, offs], [out])
-        return op("s", d, lambda q: q.activation(ap(out), ap(win).indirect(ap(offs)), ACT.Copy), [win, offs], [out])
+        def fn(q):
+            return [q.matmul_mx(ap(out), ap(a), ap(b), ap(rq), ap(rs), i == 0, i == len(ls) - 1) for i, (a, b) in enumerate(ls)][-1]
+        return op("t", len(ls) * (m + 16) * C["pe"], fn, list(ls[0]) + [rq, rs] + list(ls[-1]), [out])
 
-    def gather2(out, win, offs, engs, o0=0):
-        for i, e in enumerate(engs):
-            gather(e, vw(out, 288 * i, 288 * i + 288), win, vw(offs, o0 + 18 * i, o0 + 18 * i + 18))
+    def gather(key, out, win, offs):
+        cut = O[key]
+        for e, a, b in (("v", 0, cut), ("s", cut, offs[2] - offs[1])):
+            if a == b:
+                continue
+            o, l = vw(out[0], out[1] + 16 * a, out[1] + 16 * b), vw(offs[0], offs[1] + a, offs[1] + b)
+            d = (60 + 16 * (b - a) * C["gather"]) * CYC
+            if e == "v":
+                op(e, d, lambda q, o=o, l=l: q.tensor_copy(ap(o), ap(win).indirect(ap(l))), [win, l], [o])
+            else:
+                op(e, d, lambda q, o=o, l=l: q.activation(ap(o), ap(win).indirect(ap(l)), ACT.Copy), [win, l], [o])
+            ops[-1]["name"] = key + ":" + e
 
-    def pick(dst, src, w, offs):
+    def pick(dst, src, w, offs, at=0):
         m = 16 * len(cols(offs))
-        qo, so, qi, si = vw("q_" + dst, 0, m), vw("s_" + dst, 0, m), vw("q_" + src, 0, w), vw("s_" + src, 0, w)
+        qo, so, qi, si = vw("q_" + dst, at, at + m), vw("s_" + dst, at, at + m), vw("q_" + src, 0, w), vw("s_" + src, 0, w)
         d = (60 + m * C["gather"]) * CYC
         op("v", d, lambda q: q.tensor_copy(ap(qo).bitcast(dt.uint32), ap(qi).bitcast(dt.uint32).indirect(ap(offs))), [qi, offs], [qo])
         op("s", d, lambda q: q.activation(ap(so), ap(si).indirect(ap(offs)), ACT.Copy), [si, offs], [so])
 
-    def unpack(q, m, dst, d0, banks, engs, w=False):
-        for b in (0, 2, 1, 3):
-            if w:
-                mm(banks[b], "w", 128 * b, q, 0, m, True, False)
-            mm(banks[b], "e", 128 * b, q, 0, m, not w, True)
-            src, out = vw("ps", 512 * banks[b], 512 * banks[b] + m), vw(dst, d0 + b, d0 + 4 * m, 4)
+    def unpack(key, q, q0, m, dst, d0, w=False, back=False):
+        engs, banks = O[key][0], BANKS[O[key][1]]
+        for b in range(4):
+            mm(banks[b], "w+e" if w else "e", 128 * b, q, q0, m)["name"] = "%s*:%d" % (key, b)
+            src = vw("ps", 512 * banks[b], 512 * banks[b] + m)
+            out = vw(dst, d0 + 4 * m - 4 + b, d0 + b - 4, -4) if back else vw(dst, d0 + b, d0 + 4 * m, 4)
             if engs[b] == "v":
                 ts(out, src, 0.015625, A.mult)
             else:
                 act(out, src, ACT.Copy, scale=0.015625)
+            ops[-1]["name"] = "%s:%d" % (key, b)
 
     def dma(eng, out, in_, reads, writes, nbytes):
-        o = op(eng, 0.1, lambda q: q.dma_start(out, in_), reads, writes, kind="d", lat=0.7)
-        o["pre"], o["wire"] = 1.3, (8 * C["row"] * 0.6 + nbytes / 16 * C["byte"] * 0.6 if nbytes else 0.05)
+        o = op(eng, C["issue"], lambda q: q.dma_start(out, in_), reads, writes, kind="d", lat=C["post"])
+        o["pre"], o["wire"] = C["pre"], (8 * C["row"] + nbytes / 16 * C["byte"] if nbytes else 0.05)
 
     def send(t, pairs):
         dst = cores[(rank + 1 + t) % n]
@@ -160,246 +197,289 @@ def plan(T, topo, core, rank, C=COST, O=OPT):
         o["n"], o["pre"] = share * len(pairs), 0.0
         o["wire"] = 128 / share * (C["row"] + C["byte"] * len(cols(v)) * WIDE[SCRATCH[v[0]][2]])
 
-    nxt = {"wf": 2, "wi": 0, "off": 0, "ci": 0}
+    nxt = {"wf": 2, "off": 0}
 
-    def new(buf, m=36):
+    def new(label, m=36, buf="wf"):
         nxt[buf] += m
+        labels.append((buf, nxt[buf] - m, nxt[buf], label))
         return vw(buf, nxt[buf] - m, nxt[buf])
 
     def step(v, h, s):
         return vw(v[0], v[1] + h, v[2], s)
 
-    dma("y", T.xb[:], T.x[:], [], [vw("xb", 0, 1152)], 294912)
     dma("y", T.ub[:], T.u[:], [], [vw("ub", 0, 512)], 131072)
+    dma("y", T.x0[:], T.x[:], [], [vw("x0", 0, 1152)], 294912)
     dma("y", T.q_w[:].bitcast(dt.uint8), T.wc[:], [], [vw("q_w", 0, 512)], 262144)
     dma("y", T.s_w[:], T.ws[:], [], [vw("s_w", 0, 512)], 65536)
 
-    P, R, R8, TT, I0, K7, C3, PEN, KH0, KH1, EX, T576, TM32, KB, KX0, KX1 = [vw("pc", i, i + 1) for i in range(16)]
+    K16, J4, EL, K8, C8, R8, P112, N2, B2, B3, B4, KB, KN = [vw("pc", i, i + 1) for i in range(13)]
     p = vw("pi", 0, 1)
-    iota(p, [[0, 1]], 0, 1)
-    ts(vw("pi", 1, 2), p, 15, A.bitwise_and)
-    ts(vw("pi", 2, 3), p, 8, A.bitwise_and)
-    ts(vw("pi", 3, 4), p, 3, A.bitwise_and)
-    ts(vw("pi", 4, 5), p, 12, A.bitwise_and, 2, A.logical_shift_right)
-    ts(vw("pi", 5, 6), p, 7, A.bitwise_and)
-    ts(vw("pi", 6, 7), p, 3, A.logical_shift_right)
-    cp(vw("pc", 0, 7), vw("pi", 0, 7))
-    ts(PEN, p, 112.0, A.is_lt, 1000.0, A.mult)
-    act(KB, I0, scale=-72.0, bias=TT)
-    act(KH0, KB, bias=504.0)
-    act(KH1, KB, bias=216.0)
-    act(EX, KB, scale=-1.0 / 72, bias=-3.472)
-    act(T576, TT, bias=576.0)
-    act(TM32, TT, bias=-32.0)
-    fill(vw("c64", 0, 128), 64.0)
-    iota(vw("dep", 0, 162), [[0, 18], [1, 9]], -1)
-    for b in range(3):
-        act(vw("eb", b, 528, 4), vw("dep", 0, 132), ACT.Copy, scale=0.0)
-    for b in (2, 3):
-        act(vw("cone", b, 648, 4), vw("dep", 0, 162), ACT.Copy, scale=0.0)
-        act(vw("rich", b, 512, 4), vw("dep", 0, 128), ACT.Copy, scale=0.0)
-    fill(vw("ts0", 0, 576), 0.0)
-    fill(vw("ts2", 0, 576), 0.0)
-    fill(vw("src1", 0, 16), 0.0)
-    iota(vw("li", 0, 10), [[16, 10]], 0)
-    cp(vw("lu", 0, 8), vw("li", 0, 8))
-    ts(vw("lf", 0, 9), vw("li", 0, 9), R, A.add)
-    tt(vw("lf", 30, 39), vw("lf", 0, 9), vw("li", 0, 9), A.add)
-    ts(vw("lu", 10, 19), vw("lf", 30, 39), R8, A.add)
-    ts(vw("li", 20, 29), vw("lf", 0, 9), 1.0 / 18, A.mult, -0.472, A.add)
-    ts(vw("lf", 10, 19), vw("li", 20, 29), -143.0 / 8, A.mult)
-    tt(vw("lf", 20, 29), vw("lf", 10, 19), vw("lf", 0, 9), A.add)
-    ts(vw("lu", 20, 29), vw("lf", 20, 29), 8.0, A.mult)
-    LU, LTOP, LDM = vw("lu", 0, 8), vw("lu", 10, 19), vw("lu", 20, 29)
-    iota(vw("icp", 0, 180), [[-1, 20], [0, 9]], 17)
-    for b in range(2):
-        a0, a1 = vw("ab", 324 * b, 324 * b + 162), vw("ab", 324 * b + 162, 324 * b + 324)
-        act(a0, vw("icp", 18 * b, 18 * b + 162), ACT.Abs, scale=-1.0, bias=C3)
-        if b:
-            ts(a1, vw("dep", 0, 162), K7, A.subtract, PEN, A.subtract)
-        else:
-            ts(a1, vw("dep", 0, 162), K7, A.subtract)
-        tt(vw("cone", b, 648, 4), a0, a1, A.is_le)
-    quant("cone", vw("cone", 0, 648))
-    iota(vw("bi", 0, 162), [[-4, 18], [72, 9]], 68)
-    iota(vw("bi", 162, 198), [[8, 2], [0, 18]], -76)
-    act(vw("bc", 0, 198), vw("bi", 0, 198), scale=1.0 / 2048)
-    ev = vw("eb", 3, 515, 4)
-    op("g", 460 * CYC, lambda q: q.affine_select(ap(ev), T.c64[:], [[-1, 128]], A.is_equal, 0.0, 0, 1), [vw("c64", 0, 128)], [ev])
+    iota(vw("pi", 0, 9), [[0, 9]], 0, 1)
+    fill(vw("c64", 0, 288), 64.0)
+    fill(vw("eb", 0, 528), 0.0)
+    ev, c64 = vw("eb", 3, 515, 4), vw("c64", 0, 128)
+    op("g", 460 * CYC, lambda q: q.affine_select(ap(ev), ap(c64), [[-1, 128]], A.is_equal, 0.0, 0, 1), [c64], [ev])
     for b in range(4):
         quant("e", vw("eb", 3 - b, 515 - b), 128 * b)
+    ts(vw("pr", 0, 9), vw("pi", 0, 9), 15, A.bitwise_and)
+    ts(vw("pr", 9, 10), p, 12, A.bitwise_and)
+    ts(vw("pr", 10, 11), p, 3, A.bitwise_and)
+    ts(vw("pr", 11, 12), p, 7, A.bitwise_and)
+    ts(vw("pr", 12, 13), p, 1, A.logical_shift_right, 60, A.bitwise_and)
+    ts(vw("pr", 13, 14), p, 8, A.bitwise_and)
+    cp(vw("pc", 0, 6), vw("pr", 8, 14))
+    ts(P112, p, 112.0, A.is_ge, 2048.0, A.mult)
+    act(N2, K8, scale=-4.0, bias=-404.0)
+    j4, k2, t2, C2, N0 = vw("pc", 28, 30), vw("li", 30, 32), vw("pc", 30, 32), vw("pc", 32, 34), vw("pc", 34, 36)
+    iota(j4, [[64, 2]], 0, 4)
+    ts(k2, j4, 1.0 / 72, A.mult, -0.472, A.add)
+    ts(t2, k2, -72.0, A.mult)
+    ts(N0, k2, -4.0, A.mult, -404.0, A.add)
+    tt(C2, j4, t2, A.add)
+    act(B2, J4, scale=2.0, bias=548.0)
+    act(B4, J4, scale=-1.0, bias=EL)
+    act(B3, B4, bias=-548.0)
+    act(KB, J4, scale=-18.0, bias=EL)
+    act(KN, R8, scale=18.0, bias=K8)
+    CA, CB, KC, KD, B5, B6, B7, B8 = [vw("pc", i, i + 1) for i in range(20, 28)]
+    act(CA, K16, bias=-31.97)
+    act(CB, K16, bias=-15.97)
+    act(KC, K16, bias=-400.0)
+    act(KD, K16, bias=-384.0)
+    act(B6, J4, scale=-2.0, bias=428.0)
+    act(B7, J4, scale=-2.0, bias=396.0)
+    act(B8, J4, scale=3.0, bias=EL)
+    iota(vw("icp", 0, 180), [[-1, 20], [0, 9]], 17)
+    iota(vw("dep", 0, 180), [[0, 20], [4, 9]], 400)
+    for b in (2, 3):
+        sfill(vw("cone0", b, 648, 4), 0.0)
+        sfill(vw("cone1", b, 648, 4), 0.0)
+        sfill(vw("rich", b, 512, 4), 0.0)
+    for h in range(2):
+        sfill(vw("win", 288 * h, 288 * h + 288), 0.0)
+    LU, LD0, LD2, LN = vw("lu", 0, 8), vw("lu", 8, 17), vw("lu", 18, 27), vw("lu", 28, 46)
+    iota(vw("li", 0, 18), [[16, 18]], 0)
+    cp(LU, vw("li", 0, 8))
+    j, k = new("j", 9), vw("li", 20, 29)
+    tt(j, vw("li", 0, 9), vw("pr", 0, 9), A.add)
+    ts(k, j, 1.0 / 18, A.mult, -0.472, A.add)
+    for out, z in ((LD0, 16), (LD2, 8)):
+        t0, t1 = new("ka%d" % z, 9), new("kb%d" % z, 9)
+        ts(t0, k, (1.0 - 18 * z) / z, A.mult)
+        tt(t1, t0, j, A.add)
+        ts(out, t1, float(z), A.mult)
+    ts(LN, vw("li", 0, 18), 0.5, A.mult, KN, A.add)
+    def away(at, m, c):
+        a0, a1 = vw("ab", at, at + m), vw("ab", at + m, at + 2 * m)
+        act(a0, vw("icp", 0, m), ACT.Abs, scale=-4.0, bias=c)
+        scan(a1, a0, vw("dep", 0, m), 0.0, A.max, A.subtract)
+        return a1[1]
 
-    def const(al, be, ga, deep=True):
-        v = new("ci")
-        iota(v, [[al, 18], [be, 2]], ga)
-        if not deep:
-            return v
-        out = vw("cc", v[1], v[2])
-        act(out, v, bias=I0)
-        return out
+    for b, weight in enumerate((4096.0, P112)):
+        at = away(324 * b, 162, vw("pc", C2[1] + b, C2[1] + b + 1))
+        ts(vw("cone0", b, 648, 4), vw("ab", at, at + 162), vw("pc", N0[1] + b, N0[1] + b + 1), A.is_le, weight, A.mult)
+    quant("cone0", vw("cone0", 0, 648))
+    at = away(648, 180, C8)
+    for b, weight in enumerate((4096.0, P112)):
+        ts(vw("cone1", b, 648, 4), vw("ab", at + 18 * b, at + 18 * b + 162), N2, A.is_le, weight, A.mult)
+    quant("cone1", vw("cone1", 0, 648))
+    FORMS = {"deep": (0, 72, 4), "nat": (198, 4, 64), "flat": (396, 4, 0)}
+    for at, per, each in FORMS.values():
+        if each:
+            iota(vw("bc", at, at + 162), [[-each, 18], [per, 9]], 17 * each)
+            sfill(vw("bc", at + 162, at + 180), float(-per - each))
+            sfill(vw("bc", at + 180, at + 198), float(each - per))
+        else:
+            sfill(vw("bc", at + 162, at + 198), float(-per))
+    PROG = {"x2t": (0, 4), "in": (144, 4), "top": (288, 4), "low": (432, 4), "x2b": (576, 5)}
+
+    def slot(buf, name, s):
+        at, steps = PROG[name]
+        return vw(buf, at + s, at + 36 * steps, steps)
+
+    for name, (at, steps) in PROG.items():
+        labels.extend((buf, at, at + 36 * steps, buf + name) for buf in "pm")
+    up, down, rows, edge = new("up"), new("down"), new("rows"), new("edge")
+    iota(up, [[32, 18], [-16, 2]], 0)
+    iota(down, [[-2, 18], [288, 2]], 0)
+    iota(rows, [[4, 18], [-288, 2]], 504)
+    act(edge, rows, bias=KB)
+    act(slot("p", "top", 2), down, scale=1.0 / 9, bias=B2)
+    act(slot("p", "top", 3), up, bias=B3)
+    tab = [new("tab%d" % i) for i in range(7)]
+    iota(tab[0], [[64, 18], [0, 2]], 64)
+    iota(tab[3], [[96, 18], [-16, 2]], -628)
+    act(tab[1], tab[3], bias=B4)
+    iota(tab[6], [[32, 18], [16, 2]], -416)
+    act(tab[5], tab[6], bias=K16)
+    sfill(vw("win1", 0, 16), 0.0)
+    iota(tab[4], [[-32, 18], [48, 2]], 1412)
+    act(tab[2], tab[4], bias=B8)
+    act(slot("p", "x2t", 2), tab[0], scale=-0.5, bias=1120.0)
+    iota(slot("p", "x2b", 2), [[-32, 18], [0, 2]], 1088)
+    sfill(vw("m", 290, 576, 4), 1.0 / 18)
+    for (out, val), e in zip(((slot("m", "x2t", 1), -2.0), (slot("m", "x2b", 1), -2.0), (vw("m", 0, 288, 4), 0.0), (vw("m", 288, 576, 4), 0.0),
+                              (slot("m", "x2b", 0), 0.0), (slot("m", "in", 1), 1.0), (slot("p", "in", 3), 0.0),
+                              (vw("m", 289, 576, 4), 544.0 * 18), (slot("m", "top", 3), 1.0)), O["fill"]):
+        sfill(out, val, e)
 
     quant("u", vw("ub", 0, 512))
     pick("up", "u", 128, LU)
 
-    def cuts(q):
+    def sums(r):
+        i = min(r, 1)
         for b in range(2):
-            mm(4 + b, q, 16 * b, "up", 0, 128)
+            mm(4 + b, "x%d" % r if r else "d0", 16 * b, "up", 0, 128)["name"] = "score%d:%d" % (r, b)
         for b in range(2):
-            ts(vw("rich", b, 512, 4), vw("ps", 512 * (4 + b), 512 * (4 + b) + 128), 0.0, A.is_gt, 0.5, A.subtract)
-        quant("rich", vw("rich", 0, 512))
-        mm(4, "rich", 0, "cone", 0, 162)
-        return reach(0)
+            out, src = vw("rich", b, 512, 4), vw("ps", 512 * (4 + b), 512 * (4 + b) + 128)
+            if b == 1:
+                act(out, src, ACT.Sign, bias=-1e-37)
+            else:
+                ts(out, src, 0.0, A.is_gt, 0.5, A.subtract)
+            ops[-1]["name"] = "rich%d:%d" % (r, b)
+        quant("rich", vw("rich", 0, 512))["name"] = "q_rich%d:0" % r
+        mm(4, "rich", 0, "cone%d" % i, 0, 162)["name"] = "sums%d:0" % r
 
-    def reach(k):
-        m, f, a = new("wf", 162), new("wf", 18), new("wf", 18)
-        scan(m, vw("ps", 2048, 2048 + 162), vw("bc", k, k + 162), 8.0, A.max, A.min)
-        scan(f, vw("bc", k + 162, k + 180), step(m, 8, 9), -1.0, A.add, A.max)
-        scan(a, vw("bc", k + 180, k + 198), vw("wf", f[2] - 1, f[1] - 1, -1), -1.0, A.add, A.max)
+    def reach(form, outs, r=""):
+        at = FORMS[form][0]
+        m, f = new("m" + form + r, 162), new("f" + form + r, 18)
+        caps = vw("bc", at, at + 162) if FORMS[form][2] else vw("dep", 0, 162)
+        scan(m, vw("ps", 2048, 2048 + 162), caps, 5000.0, A.max, A.min)
+        scan(f, vw("bc", at + 162, at + 180), step(m, 8, 9), -1000.0, A.add, A.max)
+        for out in outs:
+            scan(out, vw("bc", at + 180, at + 198), vw("wf", f[2] - 1, f[1] - 1, -1), -1000.0, A.add, A.max)
+
+    def run(name, terms=None):
+        at, steps = PROG[name]
+        y, pt = new("run" + name, 36 * steps), PROG[terms or name][0]
+        scan(y, vw("m", at, at + 36 * steps), vw("p", pt, pt + 36 * steps), 0.0, A.mult, A.add)
+        return step(y, steps - 1, steps)
+
+    def to_off(y, base, label):
+        out = new(label, 36, "off")
+        ts(out, y, base, A.add)
+        return out
+
+    def tops_out(r, lst, w):
+        pick("d%d" % r, "x%d" % r, w, lst)
+        send(r, [(vw("q_d%d" % r, 0, 144), vw("q_l%d" % r, 0, 144))])
+        send(r, [(vw("s_d%d" % r, 0, 144), vw("s_l%d" % r, 0, 144))])
+
+    def slots_out(r):
+        o, a = "o%d" % r, new("adeep%d" % r, 18)
+        reach("deep", [a], str(r))
+        for h in range(2):
+            ts(vw(o, h, 36, 2), a, KB, A.add, 504.0 - 288 * h, A.add)
+        send(r, [(vw(o, 0, 36), vw("l" + o, 0, 36))])
         return a
 
-    def slot_list(a, o):
-        for h, k in enumerate((KH0, KH1)):
-            ts(vw(o, h, 36, 2), a, 2048.0, A.mult, k, A.add)
-
-    def unlist(o):
-        out = new("wi")
-        ts(out, vw(o, 0, 36), 1.0 / 72, A.mult, EX, A.add)
-        return out
-
-    def add(a, b, o=A.add):
-        out = new("wf")
-        tt(out, a, b, o)
-        return out
-
-    def sub(a, b):
-        return add(a, b, A.subtract)
-
-    def mul(a, b):
-        return add(a, b, A.mult)
-
-    def to_off(col, base, dst=None, h0=0):
-        if dst is None:
-            out = new("off")
-            ts(out, col, 4.0, A.mult, base, A.add)
-            return out
-        for h in range(2):
-            ts(step(dst, h0 + h, 4), step(col, h, 2), 4.0, A.mult, base, A.add)
-        return dst
-
-    def step_of(s, v):
-        out = new("wf")
-        ts(out, s, 0.0, A.is_ge, v, A.mult)
-        return out
-
-    VS = "vs"
-    SETA = (0, 1, 2, 3)
-    BK = (SETA, (6, 7, 7, 6))
-    iota(vw("bi", 198, 360), [[-64, 18], [4, 9]], 1088)
-    iota(vw("bi", 360, 396), [[128, 2], [0, 18]], -68)
-    act(vw("bc", 198, 396), vw("bi", 198, 396), scale=1.0 / 4096)
-    new("ci")
-    act(KX0, I0, scale=4.0, bias=TT)
-    act(KX1, KX0, bias=16.0)
-    CS, CSE, CT, CD, CG = const(0, 8, -12), const(0, 4, -8), const(8, 8, -4), const(-8, 4, 137), const(-8, 0, 272, False)
-
-    quant("x0", vw("xb", 0, 1152))
-    pick("t0", "x0", 288, LTOP)
-    send(0, [(vw("q_t0", 0, 144), vw("q_l0", 0, 144))])
-    send(0, [(vw("s_t0", 0, 144), vw("s_l0", 0, 144))])
-    a0 = cuts("t0")
-    y0 = reach(198)
-    slot_list(a0, "o0")
-    send(0, [(vw("o0", 0, 36), vw("lo0", 0, 36))])
-    unpack("x0", 288, "src0", 0, SETA, O["e_t0"])
-    h0 = unlist("o0")
-    o1 = new("off")
-    for h, k in enumerate((KX0, KX1)):
-        ts(step(o1, h, 2), y0, 4096.0, A.mult, k, A.add)
-    gather2("x1t", vw("src0", 0, 1152), "off", VS, o1[1])
-    quant("x1t", vw("x1t", 0, 576))
-    a1 = cuts("x1t")
-    h1 = vw("a1", 0, 36)
-    for h in range(2):
-        ts(step(h1, h, 2), a1, 2048.0 / 72, A.mult, 4.0 - 4 * h - 0.472, A.add)
-    fl = new("wf")
-    ts(fl, h1, -5.0, A.add, I0, A.is_ge)
+    quant("x0", vw("x0", 0, 1152))
+    tops_out(0, LD0, 288)
+    sums(0)
+    slots_out(0)
+    n0, o1, near = new("n0", 18), new("ox1t", 36, "off"), new("near")
+    reach("nat", [n0])
+    unpack("t0", "x0", 0, 288, "src0", 0)
     quant("f0", vw("src0", 0, 1152))
-    unpack("f0", 288, "src1", 16, BK[O["b_f0"]], O["e_f0"])
-    pick("d0", "l0", 144, LDM)
-    unpack("d0", 144, "ts0", 576, SETA, O["e_ts0"])
-    gather2("b0", vw("ts0", 0, 1152), "lo0", VS)
+    unpack("f0", "f0", 0, 288, "src1", 0)
+    unpack("w0", "l0", 0, 144, "win", 576)
+    for h in range(2):
+        ts(step(o1, h, 2), n0, K16, A.add, 16.0 * h, A.add)
+        act(step(near, h, 2), n0, bias=(KC, KD)[h])
+    gather("x1t", vw("x1", 0, 576), vw("src0", 0, 1152), o1)
+    quant("x1", vw("x1", 0, 576))
+    send(1, [(vw("q_x1", 0, 144), vw("q_l1", 0, 144))])
+    send(1, [(vw("s_x1", 0, 144), vw("s_l1", 0, 144))])
+    sums(1)
+    n1 = new("n1")
+    reach("flat", [step(n1, h, 2) for h in range(2)])
+    a1, z1, cut = new("a1"), new("z1"), slot("m", "in", 3)
+    for h in range(2):
+        ts(step(cut, 4 * h, 8), step(n1, h, 2), J4, A.add, 430.0 - 16 * h, A.is_ge)
+        ts(vw("o1", 36 + h, 72, 2), step(n1, h, 2), J4, A.subtract, 30.0 - 16 * h, A.add)
+    tt(a1, n1, tab[5], A.add)
+    tt(z1, a1, cut, A.mult)
+    cp(vw("o1", 0, 36), z1)
+    send(1, [(vw("o1", 0, 72), vw("lo1", 0, 72))])
+    gather("b0", vw("b0", 0, 576), vw("win", 0, 1152), vw("lo0", 0, 36))
     quant("b0", vw("b0", 0, 576))
-    g0 = unlist("lo0")
-    unpack("b0", 144, "h0", 0, SETA, "vvss", True)
+    unpack("h0", "b0", 0, 144, "h0", 0, True)
     quant("h0", vw("h0", 0, 576))
-    unpack("h0", 144, "src1", 16 + 1152, SETA, "vvss")
+    unpack("dh0", "h0", 0, 144, "src1", 1152)
 
-    ob1 = to_off(mul(add(h1, sub(h0, const(-16, -4, 5))), fl), TT)
-    gather2("b1", vw("src1", 0, 16 + 1152), "off", O["e_b1"], ob1[1])
-    pk, npk = add(h0, const(0, 12, -24)), new("wf")
-    ts(npk, pk, -1.0, A.mult)
-    lim = add(g0, sub(npk, const(0, -4, 4, False)))
-    n1 = add(h1, add(pk, const(16, 0, 16, False)))
-    w1 = add(h1, const(-24, 8, 253))
-    kept = add(mul(add(h1, lim, A.is_lt), n1), mul(add(h1, npk, A.is_ge), CG))
-    ot = to_off(sub(kept, mul(add(h1, lim, A.is_ge), w1)), TT)
-    own = sub(w1, CG)
-    uu = add(n1, own)
-    gather2("x2t", vw("src1", 16, 16 + 1728), "off", VS, ot[1])
-    u16, h8 = new("wf"), new("wf")
-    ts(u16, uu, 16.0, A.add)
-    ts(h8, h1, 8.0, A.add)
-    dl = add(u16, mul(add(h8, npk, A.is_ge), CG))
-    colp = sub(mul(add(h8, lim, A.is_lt), dl), own)
-    k16 = add(h1, CS)
-    mk = step_of(k16, 1.0)
-    evp = sub(h0, const(-16, 0, -11))
-    base = add(colp, mul(mk, sub(evp, colp)))
-    de = mul(mk, sub(add(k16, const(8, 0, 440, False)), evp))
-    k16e = add(h1, CSE)
+    deep, far, got = new("deep"), new("far"), new("got")
+    tt(deep, tab[0], near, A.subtract)
+    for h, c in enumerate((CA, CB)):
+        ts(step(got, h, 2), vw("lo0", h, 36, 2), 1.0 / 18, A.mult, c, A.add)
+    tt(far, got, deep, A.add)
+
+    def through(name, a):
+        tt(slot("m", name, 2), a, far, A.is_ge)
+        tt(slot("m", name, 3), a, deep, A.is_ge)
+
+    tt(slot("p", "x2t", 1), near, tab[1], A.add)
+    for s in (0, 3):
+        tt(slot("p", "x2t", s), n1, near, A.add)
+    through("x2t", n1)
+    gather("x2t", vw("x2", 0, 576), vw("src1", 0, 1728), to_off(run("x2t"), 0.0, "ox2t"))
+    quant("x2", vw("x2", 0, 576))
+    unpack("w1", "l1", 0, 144, "win1", 16)
+    gather("b1", vw("b1", 0, 576), vw("win1", 0, 592), vw("lo1", 0, 36))
     quant("b1", vw("b1", 0, 576))
-    send(1, [(vw("q_b1", 0, 144), vw("q_l1", 0, 144))])
-    send(1, [(vw("s_b1", 0, 144), vw("s_l1", 0, 144)), (h1, vw("la1", 0, 36))])
-    quant("x2t", vw("x2t", 0, 576))
+    low = new("low")
+    act(low, n1, bias=32.0)
+    through("x2b", low)
+    for s, more in ((0, 32.0), (1, 0.0), (3, 32.0)):
+        act(slot("p", "x2b", s), slot("p", "x2t", s), bias=more)
+    act(slot("m", "x2b", 4), cut, scale=-1.0, bias=1.0)
+    act(slot("p", "in", 0), n1, ACT.Copy)
+    tt(slot("p", "in", 1), tab[2], near, A.subtract)
+    for h, c in enumerate((B6, B7)):
+        act(step(slot("p", "in", 2), 4 * h, 8), step(near, h, 2), bias=c)
 
-    send(2, [(vw("q_x2t", 0, 144), vw("q_l2", 0, 144))])
-    send(2, [(vw("s_x2t", 0, 144), vw("s_l2", 0, 144))])
-    a2 = cuts("x2t")
-    slot_list(a2, "o2")
-    send(2, [(vw("o2", 0, 36), vw("lo2", 0, 36))])
-    unpack("l1", 144, "src1", 16 + 1728, BK[O["b_h1"]], O["e_h1"], True)
-    unpack("x2t", 144, "src2", 0, BK[O["b_t2t"]], O["e_t2t"])
-    ob = to_off(add(base, mul(add(k16e, vw("la1", 0, 36), A.is_lt), de)), TM32)
-    gather2("x2b", vw("src1", 16, 16 + 2304), "off", O["e_x2b"], ob[1])
-    quant("x2b", vw("x2b", 0, 576))
-    pick("d2", "l2", 144, LDM)
-    unpack("d2", 144, "ts2", 576, BK[O["b_ts2"]], O["e_ts2"])
-    unpack("x2b", 144, "src2", 576, BK[O["b_t2b"]], O["e_t2b"])
-    dma("y", T.vb[:], T.v[:], [vw(O["vat"], 0, 36)], [vw("vb", 0, 512)], 131072)
+    tops_out(2, LD2, 144)
+    sums(2)
+    a2 = slots_out(2)
+    for h in range(2):
+        act(step(slot("p", "top", 1), 4 * h, 8), a2, ACT.Copy)
+    tt(slot("p", "top", 0), slot("p", "top", 1), edge, A.is_gt)
+    unpack("h1", "b1", 0, 144, "src1", 1728, True, True)
+    unpack("t2t", "x2", 0, 144, "src2", 0)
+    got = new("got1")
+    cp(got, vw("lo1", 36, 72))
+    tt(slot("m", "in", 2), n1, got, A.is_lt)
+    act(slot("p", "x2b", 4), run("in"), ACT.Copy)
+    gather("x2b", vw("x2", 576, 1152), vw("src1", 0, 2304), to_off(run("x2b"), 0.0, "ox2b"))
+    quant("x2", vw("x2", 576, 1152), 144)
+    unpack("w2", "l2", 0, 144, "win", 576)
+    unpack("t2b", "x2", 144, 144, "src2", 576)
+    dma("y", T.vb[:], T.v[:], [vw(O["vat"], 0, 36)] if O["vat"] else [], [vw("vb", 0, 512)], 131072)
     quant("v", vw("vb", 0, 512))
-    h2 = unlist("o2")
-    cp(vw("oaf", 0, 18), step(h2, 1, 2))
+    ts(vw("li", 32, 50), a2, 1.0 / 72, A.mult, -0.472, A.add)
+    cp(vw("oaf", 0, 18), vw("li", 32, 50))
     dma("y", T.oa[:], T.oaf[0:128:16, :], [vw("oaf", 0, 18)], [], 0)
-    top2 = add(add(h2, CT), step_of(add(h2, CS), 136.0))
-    o3 = new("off", 72)
-    to_off(top2, TT, o3, 0)
-    se2, d2 = add(h2, CSE), add(top2, CD)
-    gather2("b2", vw("ts2", 0, 1152), "lo2", VS)
+    gather("b2", vw("b2", 0, 576), vw("win", 0, 1152), vw("lo2", 0, 36))
     quant("b2", vw("b2", 0, 576))
-    unpack("b2", 144, "src2", 1152, SETA, "vvss", True)
-    to_off(sub(mul(add(se2, unlist("lo2"), A.is_lt), d2), CD), T576, o3, 2)
+    unpack("h2", "b2", 0, 144, "src2", 1152, True)
+    got = new("got2")
+    ts(got, vw("lo2", 0, 36), 36.0, A.add)
+    tt(slot("m", "low", 3), slot("p", "top", 1), got, A.is_lt)
 
-    for i, e in enumerate(VS):
-        gather(e, vw("x3", 576 * i, 576 * i + 576), vw("src2", 0, 1728), vw("off", o3[1] + 36 * i, o3[1] + 36 * i + 36))
-    for i in range(2):
+    for i, (key, lst) in enumerate((("x3t", to_off(run("top"), 0.25, "ox3t")), ("x3b", to_off(run("low", "top"), 576.25, "ox3b")))):
+        gather(key, vw("x3", 576 * i, 576 * i + 576), vw("src2", 0, 1152 + 576 * i), lst)
         quant("x3", vw("x3", 576 * i, 576 * i + 576), 144 * i)
         mm(4 + i, "v", 0, "x3", 144 * i, 144)
-    dma("y", T.oc[:], T.q_x3[:].bitcast(dt.uint8), [vw("q_x3", 0, 288)], [], 150000)
+        src, out = vw("ps", 512 * (4 + i), 512 * (4 + i) + 144), T.yb[:, :, 8 * i:8 * i + 8]
+        if O["y"][i] == "v":
+            op("v", vdur(144), lambda q, s=src, o=out: q.tensor_copy(o, ap(s)), [src], [vw("yb", i, i + 1)])
+        else:
+            op("s", vdur(144), lambda q, s=src, o=out: q.activation(o, ap(s), ACT.Copy), [src], [vw("yb", i, i + 1)])
+    for a, b in ((0, 10), (10, 18)):
+        pick("last", "x3", 288, vw("lu", LN[1] + a, LN[1] + b), 16 * a)
+        dma("y", T.oc[:, 64 * a:64 * b], T.q_last[:, 16 * a:16 * b].bitcast(dt.uint8), [vw("q_last", 16 * a, 16 * b)], [], 8192 * (b - a))
     for k in range(4):
-        dma("y" if k < 2 else "s", T.osc[4 * k:4 * k + 4, :], T.s_x3[32 * k:32 * k + 4, :], [vw("s_x3", 0, 288)], [], 0)
-    act(vw("yb", 0, 144), vw("ps", 2048, 2048 + 144), ACT.Copy)
-    cp(vw("yb", 144, 288), vw("ps", 2560, 2560 + 144))
-    dma("s", T.y[:], T.yb[:], [vw("yb", 0, 288)], [], 150000)
+        dma(O["out"][k], T.osc[4 * k:4 * k + 4, :], T.s_last[32 * k:32 * k + 4, :], [vw("s_last", 0, 288)], [], 0)
+    dma(O["out"][4], T.y[:], T.yb[:], [vw("yb", 0, 2)], [], 150000)
     return ops
 
 
@@ -423,13 +503,101 @@ def depend(ops):
         o["deps"] = deps
 
 
+def place(busy, t, dur):
+    for a, b in busy:
+        if t < b and t + dur > a:
+            t = b
+    busy.append((t, t + dur))
+    busy.sort()
+    return t
+
+
+def order(ops, C=COST, late=None):
+    late = LATE if late is None else late
+    named = {o["name"]: o for o in ops}
+    for o in ops:
+        o["behind"] = set()
+    for row in late.get("rows", ROWS):
+        row = [named[x if ":" in x else x + ":0"] for x in row.split()]
+        for e in "vstgy":
+            mine = [o for o in row if o["eng"] == e]
+            for a, b in zip(mine, mine[1:]):
+                b["behind"].add(a["id"])
+    after = [[] for o in ops]
+    for o in ops:
+        o["ahead"], o["need"] = None, len(o["deps"] | o["behind"])
+        for j in o["deps"] | o["behind"]:
+            after[j].append(o)
+
+    def ahead(o):
+        if o["ahead"] is None:
+            tail = o["lat"] + o.get("pre", 0.0) + o.get("wire", 0.0)
+            o["ahead"] = o["dur"] + late.get(o["name"] + "+", 0.0) + max(
+                [tail] + [ahead(x) + (tail + C["wake"] if o["id"] in x["deps"] else 0.0) for x in after[o["id"]]])
+        return o["ahead"]
+
+    for o in reversed(ops):
+        ahead(o)
+    free, done, wire, seq, first = {}, {}, [], [], [C["first"]]
+    ready = [o for o in ops if not o["need"]]
+    for o in ready:
+        o["from"] = late.get(o["name"], 0.0)
+    while ready:
+        o = min(ready, key=lambda o: (max(o["from"], free.get(o["eng"], 0.0)), -o["ahead"]))
+        t = max(o["from"], free.get(o["eng"], 0.0))
+        o = max([x for x in ready if x["eng"] == o["eng"] and x["from"] <= t + C["patience"] * o["dur"]], key=lambda x: x["ahead"])
+        t = free[o["eng"]] = max(t, o["from"]) + o["dur"] + (first.pop() if o["kind"] == "r" and first else 0.0)
+        if o["kind"] != "c":
+            t = place(wire, t + o["pre"], o["wire"]) + o["wire"] + o["lat"]
+        done[o["id"]] = t
+        seq.append(o)
+        ready.remove(o)
+        for x in after[o["id"]]:
+            x["need"] -= 1
+            if not x["need"]:
+                x["from"] = max([late.get(x["name"], 0.0)] + [done[j] + C["wake"] for j in x["deps"]])
+                ready.append(x)
+    return seq
+
+
+def settle(ops, seq, C=COST):
+    first = next(o for o in seq if o["kind"] == "r")
+    after = [[] for o in ops]
+    for o in ops:
+        o["hold"] = o["dur"] * (C["busy"] if o["kind"] == "c" else 1.0) + (C["first"] if o is first else 0.0)
+        o["tail"] = o["lat"] + o.get("pre", 0.0) + o.get("wire", 0.0)
+        for j in o["deps"] | o["behind"]:
+            after[j].append(o)
+    for sweep in range(2):
+        busy, back = {}, {}
+        for o in reversed(seq):
+            t = max([o["tail"]] + [back[x["id"]] + (C["pause"] + o["tail"] if o["id"] in x["deps"] else 0.0) for x in after[o["id"]]])
+            if o is first:
+                t = max([t] + [back[x["id"]] for x in ops if x["kind"] == "r" and x is not o])
+            back[o["id"]] = place(busy.setdefault(o["eng"], []), t, o["hold"]) + o["hold"]
+        busy, start, done = {}, {}, {}
+        for o in sorted(seq, key=lambda o: -back[o["id"]]):
+            t = max([start.get(first["id"], 0.0) if o["kind"] == "r" else 0.0] + [done[j] + C["pause"] for j in o["deps"]]
+                    + [start[j] + ops[j]["hold"] for j in o["behind"]])
+            start[o["id"]] = t = place(busy.setdefault(o["eng"], []), t, o["hold"])
+            t += o["hold"]
+            if o["kind"] != "c":
+                t = place(busy.setdefault("wire", []), t + o["pre"], o["wire"]) + o["wire"] + o["lat"]
+            done[o["id"]] = t
+        seq = sorted(seq, key=lambda o: start[o["id"]])
+    return seq
+
+
 def rank_program(g, core, T, topo):
     rank = T.rank_of(core)
     if rank is None:
         return
     ops = plan(T, topo, core, rank)
     depend(ops)
-    seq = [ops[i] for i in ORDER]
+    for o in ops:
+        if o["kind"] == "r":
+            o["lat"], o["wire"] = o["lat"] * COST["slow"], o["wire"] * COST["slow"]
+    seq = settle(ops, order(ops))
     queue = {"v": g.vector, "s": g.scalar, "t": g.tensor, "g": g, "y": g.sync}
     known, count = {e: {} for e in queue}, {e: 0 for e in queue}
     for i, o in enumerate(seq):

from concourse.bass import DstId, RemoteDMATransfer
from concourse.mybir import dt, AluOpType, ActivationFunctionType

BF, F32, I32, U16, FP, U8 = "bfloat16", "float32", "int32", "uint16", "float8_e4m3fn_x4", "uint8"
SCRATCH = {"ps": ("psum", [128, 4096], F32), "yb": ("sbuf", [128, 18, 16], F32)}
for _n, _w in (("ub", 512), ("vb", 512), ("x0", 1152), ("x1", 576), ("x2", 1152), ("x3", 1152), ("src0", 1152), ("src1", 2320),
               ("src2", 1728), ("win", 1152), ("win1", 592), ("b0", 576), ("b1", 576), ("b2", 576), ("h0", 576), ("rich", 512), ("cone0", 648),
               ("cone1", 648), ("eb", 528), ("c64", 288), ("icp", 252), ("dep", 252), ("ab", 1008)):
    SCRATCH[_n] = ("sbuf", [128, _w], BF)
for _n, _w in (("u", 128), ("up", 128), ("v", 128), ("w", 512), ("e", 512), ("cone0", 162), ("cone1", 162), ("rich", 128),
               ("x0", 288), ("x1", 144), ("x2", 288), ("x3", 288), ("last", 288), ("d0", 144), ("d1", 144), ("d2", 144), ("l0", 144),
               ("l1", 144), ("l2", 144), ("b0", 144), ("b1", 144), ("b2", 144), ("f0", 288), ("h0", 144)):
    SCRATCH["q_" + _n] = ("sbuf", [128, _w], FP)
    SCRATCH["s_" + _n] = ("sbuf", [128, _w], U8)
for _n, _w, _d in (("pi", 9, I32), ("pr", 15, I32), ("pc", 36, F32), ("bc", 792, F32), ("li", 50, I32), ("lu", 48, U16),
                   ("wf", 3000, F32), ("p", 756, F32), ("m", 756, F32),
                   ("off", 288, U16), ("o0", 36, U16), ("o1", 72, U16), ("o2", 36, U16), ("lo0", 36, U16), ("lo1", 72, U16),
                   ("lo2", 36, U16), ("oaf", 18, F32)):
    SCRATCH[_n] = ("sbuf", [128, _w], _d)

SEMAPHORES = ["cv", "cs", "ct", "cg", "sent"] + ["dm%d" % i for i in range(16)] + ["ar%d" % i for i in range(10)]

A = AluOpType
ACT = ActivationFunctionType
WIDE = {BF: 2, F32: 4, I32: 4, U16: 2, FP: 4, U8: 1}
COST = {"cyc": 0.00088, "gather": 1.56, "wake": 0.25, "pe": 0.00055, "call": 0.2, "far": 0.5, "row": 0.015, "byte": 0.00004,
        "first": 0.8, "issue": 0.2, "pre": 0.45, "post": 0.3, "patience": 0.5, "pause": 0.2, "busy": 1.1, "slow": 1.2}
OPT = {"t0": ("ssss", 0), "w0": ("ssvs", 6), "h0": ("svss", 0), "f0": ("ssss", 1), "dh0": ("sssv", 0), "t2t": ("ssss", 1),
       "h1": ("ssss", 0), "w1": ("ssss", 0), "w2": ("svvs", 4), "t2b": ("ssvs", 4), "h2": ("svsv", 0),
       "x1t": 18, "b0": 18, "b1": 10, "x2t": 18, "x2b": 18, "b2": 18, "x3t": 18, "x3b": 18, "y": "ss", "fill": "sgsggsggg",
       "vat": "lo0", "out": "yyyss"}
BANKS = ((0, 1, 2, 3), (6, 7, 6, 7), (0, 1, 0, 1), (2, 3, 2, 3), (4, 5, 6, 7), (0, 1, 6, 7), (2, 3, 4, 5), (6, 7, 0, 1))
NB = len(BANKS)
LATE = {"o1:0+": 0.3, "dh0*:1+": -0.5, "deep:0": 9.3, "q_e:384": 5.2}
ROWS = ["pi li pc:28 bc icp dep eb:3 bc:198 tab0 s_l0 q_l0 lo0 tab3 tab6 q_l1 s_l1 min:1 pin:3 px2b:2 mx2b:1 mx2b tab4 rows up down mtop"
        " mtop:1 mtop:3 lo1",
        "c64 eb pr q_x0 q_u q_d0 rich0 q_cone0 q_rich0 mdeep0 mnat fdeep0 fnat adeep0 n0 o0 o0:1 ox1t ox1t:1 x1t:v q_f0 q_x1 b0:v"
        " rich1 q_b0 q_rich1 mflat fflat n1:1 n1 q_h0 px2t mx2t:2 mx2t:3 runx2t o1 ox2t"
        " x2t:v q_x2 q_d2 rich2 q_rich2 got1 b1:v min:2 mdeep2 runin q_b1 fdeep2 adeep2 runx2b o2 o2:1 ox2b runtop"
        " x2b:v q_x2:144 b2:v q_b2 x3t:v x3b:v q_x3:144 q_last:160 q_last", "s_last yb:1 s_last:160",
        "s_d0 s_up rich0:1 x1t:s w0:0 w0:3 b0:s rich1:1 f0:0 h0:0 f0:1 x2t:s w1:3 s_d2 rich2:1 b1:s t2t:0",
        "score0 score0:1 w0*:3 f0*:0 f0*:1 h0*:2 h0*:3 h0*:1", "x0 ub q_w s_w"]


def vw(name, a, b, step=1):
    return (name, a, b, step)


def cols(v):
    return range(v[1], v[2], v[3])


def plan(T, topo, core, rank, C=COST, O=OPT):
    ops = []
    cores = T.cores
    n = len(cores)
    CYC = C["cyc"]

    def ap(v):
        return T[v[0]][:, v[1]:v[2]:v[3]] if v[3] != 1 else T[v[0]][:, v[1]:v[2]]

    labels = []

    def name_of(v, reads):
        if v[0] == "ps":
            return "%s:%d*%s:%d" % (reads[0][0][2:], reads[0][1], reads[2][0][2:], reads[2][1])
        for buf, a, b, label in labels:
            if buf == v[0] and a <= min(v[1], v[2] - v[3]) < b:
                return "%s:%d" % (label, v[1] - a)
        return "%s:%d" % v[:2]

    def op(eng, dur, fn, reads, writes, kind="c", lat=0.0, acc=False):
        ops.append({"eng": eng, "dur": dur, "fn": fn, "r": [v for v in reads if isinstance(v, tuple)], "w": list(writes),
                    "kind": kind, "lat": lat, "acc": acc, "id": len(ops),
                    "name": name_of(writes[0], reads) if writes else "out%d" % len(ops)})
        while any(o["name"] == ops[-1]["name"] for o in ops[:-1]):
            ops[-1]["name"] += "'"
        return ops[-1]

    def sc(x):
        return ap(x) if isinstance(x, tuple) else x

    def narrow(*vs):
        return all(WIDE[SCRATCH[v[0]][2]] == 2 for v in vs)

    def vdur(m, f=1.0):
        return max(64, m * f) * CYC

    def ts(out, in0, s1, op0, s2=None, op1=None):
        d = vdur(len(cols(out)), 0.5 if narrow(out, in0) else 1.0)
        if op1 is None:
            return op("v", d, lambda q: q.tensor_scalar(ap(out), ap(in0), sc(s1), None, op0), [in0, s1], [out])
        return op("v", d, lambda q: q.tensor_scalar(ap(out), ap(in0), sc(s1), sc(s2), op0, op1), [in0, s1, s2], [out])

    def tt(out, a, b, o):
        return op("v", vdur(len(cols(out)), 2.0), lambda q: q.tensor_tensor(ap(out), ap(a), ap(b), o), [a, b], [out])

    def cp(out, a):
        return op("v", vdur(len(cols(out))), lambda q: q.tensor_copy(ap(out), ap(a)), [a], [out])

    def fill(out, val):
        return op("v", vdur(len(cols(out)), 0.5 if narrow(out) else 1.0), lambda q: q.memset(ap(out), val), [], [out])

    def scan(out, d0, d1, init, o0, o1):
        d = vdur(len(cols(out)), 0.5 if narrow(out, d0, d1) else 1.0)
        return op("v", d, lambda q: q.tensor_tensor_scan(ap(out), ap(d0), ap(d1), init, o0, o1), [d0, d1], [out])

    def act(out, a, func=None, bias=0.0, scale=1.0):
        f = ACT.Identity if func is None else func
        if f == ACT.Copy:
            fn = lambda q: q.activation(ap(out), ap(a), f, scale=scale) if scale != 1.0 else q.activation(ap(out), ap(a), f)
        else:
            fn = lambda q: q.activation(ap(out), ap(a), f, bias=sc(bias), scale=scale)
        return op("s", vdur(len(cols(out))), fn, [a, bias], [out])

    def sfill(out, val, eng="s"):
        if eng == "g":
            return iota(out, [[0, len(cols(out))]], int(val))
        return act(out, vw("c64", 0, len(cols(out))), ACT.Identity if val else ACT.Copy, val, 0.0)

    def iota(out, pat, base, cm=0):
        if SCRATCH[out[0]][2] != I32:
            fn = lambda q: q.iota(ap(out), pat, base, cm, allow_small_or_imprecise_dtypes=True)
        else:
            fn = lambda q: q.iota(ap(out), pat, base, cm)
        return op("g", (156 + 2 * len(cols(out))) * CYC, fn, [], [out])

    def quant(name, src, a=0):
        m = len(cols(src)) // 4
        qv, sv = vw("q_" + name, a, a + m), vw("s_" + name, a, a + m)
        return op("v", (15 + 1.06 * m) * CYC, lambda q: q.quantize_mx(ap(qv), ap(sv), ap(src)), [src], [qv, sv])

    def mm(bank, lhs, la, rhs, ra, m):
        out = vw("ps", 512 * bank, 512 * bank + m)
        ls = [(vw("q_" + x, la, la + 128), vw("s_" + x, la, la + 128)) for x in lhs.split("+")]
        rq, rs = vw("q_" + rhs, ra, ra + m), vw("s_" + rhs, ra, ra + m)

        def fn(q):
            return [q.matmul_mx(ap(out), ap(a), ap(b), ap(rq), ap(rs), i == 0, i == len(ls) - 1) for i, (a, b) in enumerate(ls)][-1]
        return op("t", len(ls) * (m + 16) * C["pe"], fn, list(ls[0]) + [rq, rs] + list(ls[-1]), [out])

    def gather(key, out, win, offs):
        cut = O[key]
        for e, a, b in (("v", 0, cut), ("s", cut, offs[2] - offs[1])):
            if a == b:
                continue
            o, l = vw(out[0], out[1] + 16 * a, out[1] + 16 * b), vw(offs[0], offs[1] + a, offs[1] + b)
            d = (60 + 16 * (b - a) * C["gather"]) * CYC
            if e == "v":
                op(e, d, lambda q, o=o, l=l: q.tensor_copy(ap(o), ap(win).indirect(ap(l))), [win, l], [o])
            else:
                op(e, d, lambda q, o=o, l=l: q.activation(ap(o), ap(win).indirect(ap(l)), ACT.Copy), [win, l], [o])
            ops[-1]["name"] = key + ":" + e

    def pick(dst, src, w, offs, at=0):
        m = 16 * len(cols(offs))
        qo, so, qi, si = vw("q_" + dst, at, at + m), vw("s_" + dst, at, at + m), vw("q_" + src, 0, w), vw("s_" + src, 0, w)
        d = (60 + m * C["gather"]) * CYC
        op("v", d, lambda q: q.tensor_copy(ap(qo).bitcast(dt.uint32), ap(qi).bitcast(dt.uint32).indirect(ap(offs))), [qi, offs], [qo])
        op("s", d, lambda q: q.activation(ap(so), ap(si).indirect(ap(offs)), ACT.Copy), [si, offs], [so])

    def unpack(key, q, q0, m, dst, d0, w=False, back=False):
        engs, banks = O[key][0], BANKS[O[key][1]]
        for b in range(4):
            mm(banks[b], "w+e" if w else "e", 128 * b, q, q0, m)["name"] = "%s*:%d" % (key, b)
            src = vw("ps", 512 * banks[b], 512 * banks[b] + m)
            out = vw(dst, d0 + 4 * m - 4 + b, d0 + b - 4, -4) if back else vw(dst, d0 + b, d0 + 4 * m, 4)
            if engs[b] == "v":
                ts(out, src, 0.015625, A.mult)
            else:
                act(out, src, ACT.Copy, scale=0.015625)
            ops[-1]["name"] = "%s:%d" % (key, b)

    def dma(eng, out, in_, reads, writes, nbytes):
        o = op(eng, C["issue"], lambda q: q.dma_start(out, in_), reads, writes, kind="d", lat=C["post"])
        o["pre"], o["wire"] = C["pre"], (8 * C["row"] + nbytes / 16 * C["byte"] if nbytes else 0.05)

    def send(t, pairs):
        dst = cores[(rank + 1 + t) % n]
        rid, pid = topo.addr(dst)[0], topo.addr(dst)[1]
        eng = topo.engines(core, dst)
        share = len(eng) // len(pairs)

        def side(v):
            return ap(v).bitcast(dt.uint8) if SCRATCH[v[0]][2] == FP else ap(v)

        def fn(q, sem, sent):
            if len(pairs) == 1:
                return q.remote_dma(side(pairs[0][1]), side(pairs[0][0]), sem, sent, pid, rid, topo.mask(core, dst))
            trs = []
            for i, (s, d) in enumerate(pairs):
                m = sum(1 << e for e in eng[share * i:share * i + share])
                trs.append(RemoteDMATransfer(dst_ids=[DstId(rid=rid, pnc=pid)], dma_engine_mask=m, remote_sem=sem, src=side(s), dst=side(d)))
            return q.remote_dma_fused(trs, local_sem=sent)
        v = pairs[0][0]
        o = op("g", C["call"], fn, [p[0] for p in pairs], [p[1] for p in pairs], kind="r", lat=C["far"])
        o["n"], o["pre"] = share * len(pairs), 0.0
        o["wire"] = 128 / share * (C["row"] + C["byte"] * len(cols(v)) * WIDE[SCRATCH[v[0]][2]])

    nxt = {"wf": 2, "off": 0}

    def new(label, m=36, buf="wf"):
        nxt[buf] += m
        labels.append((buf, nxt[buf] - m, nxt[buf], label))
        return vw(buf, nxt[buf] - m, nxt[buf])

    def step(v, h, s):
        return vw(v[0], v[1] + h, v[2], s)

    dma("y", T.ub[:], T.u[:], [], [vw("ub", 0, 512)], 131072)
    dma("y", T.x0[:], T.x[:], [], [vw("x0", 0, 1152)], 294912)
    dma("y", T.q_w[:].bitcast(dt.uint8), T.wc[:], [], [vw("q_w", 0, 512)], 262144)
    dma("y", T.s_w[:], T.ws[:], [], [vw("s_w", 0, 512)], 65536)

    K16, J4, EL, K8, C8, R8, P112, N2, B2, B3, B4, KB, KN = [vw("pc", i, i + 1) for i in range(13)]
    p = vw("pi", 0, 1)
    iota(vw("pi", 0, 9), [[0, 9]], 0, 1)
    fill(vw("c64", 0, 288), 64.0)
    fill(vw("eb", 0, 528), 0.0)
    ev, c64 = vw("eb", 3, 515, 4), vw("c64", 0, 128)
    op("g", 460 * CYC, lambda q: q.affine_select(ap(ev), ap(c64), [[-1, 128]], A.is_equal, 0.0, 0, 1), [c64], [ev])
    for b in range(4):
        quant("e", vw("eb", 3 - b, 515 - b), 128 * b)
    ts(vw("pr", 0, 9), vw("pi", 0, 9), 15, A.bitwise_and)
    ts(vw("pr", 9, 10), p, 12, A.bitwise_and)
    ts(vw("pr", 10, 11), p, 3, A.bitwise_and)
    ts(vw("pr", 11, 12), p, 7, A.bitwise_and)
    ts(vw("pr", 12, 13), p, 1, A.logical_shift_right, 60, A.bitwise_and)
    ts(vw("pr", 13, 14), p, 8, A.bitwise_and)
    cp(vw("pc", 0, 6), vw("pr", 8, 14))
    ts(P112, p, 112.0, A.is_ge, 2048.0, A.mult)
    act(N2, K8, scale=-4.0, bias=-404.0)
    j4, k2, t2, C2, N0 = vw("pc", 28, 30), vw("li", 30, 32), vw("pc", 30, 32), vw("pc", 32, 34), vw("pc", 34, 36)
    iota(j4, [[64, 2]], 0, 4)
    ts(k2, j4, 1.0 / 72, A.mult, -0.472, A.add)
    ts(t2, k2, -72.0, A.mult)
    ts(N0, k2, -4.0, A.mult, -404.0, A.add)
    tt(C2, j4, t2, A.add)
    act(B2, J4, scale=2.0, bias=548.0)
    act(B4, J4, scale=-1.0, bias=EL)
    act(B3, B4, bias=-548.0)
    act(KB, J4, scale=-18.0, bias=EL)
    act(KN, R8, scale=18.0, bias=K8)
    CA, CB, KC, KD, B5, B6, B7, B8 = [vw("pc", i, i + 1) for i in range(20, 28)]
    act(CA, K16, bias=-31.97)
    act(CB, K16, bias=-15.97)
    act(KC, K16, bias=-400.0)
    act(KD, K16, bias=-384.0)
    act(B6, J4, scale=-2.0, bias=428.0)
    act(B7, J4, scale=-2.0, bias=396.0)
    act(B8, J4, scale=3.0, bias=EL)
    iota(vw("icp", 0, 180), [[-1, 20], [0, 9]], 17)
    iota(vw("dep", 0, 180), [[0, 20], [4, 9]], 400)
    for b in (2, 3):
        sfill(vw("cone0", b, 648, 4), 0.0)
        sfill(vw("cone1", b, 648, 4), 0.0)
        sfill(vw("rich", b, 512, 4), 0.0)
    for h in range(2):
        sfill(vw("win", 288 * h, 288 * h + 288), 0.0)
    LU, LD0, LD2, LN = vw("lu", 0, 8), vw("lu", 8, 17), vw("lu", 18, 27), vw("lu", 28, 46)
    iota(vw("li", 0, 18), [[16, 18]], 0)
    cp(LU, vw("li", 0, 8))
    j, k = new("j", 9), vw("li", 20, 29)
    tt(j, vw("li", 0, 9), vw("pr", 0, 9), A.add)
    ts(k, j, 1.0 / 18, A.mult, -0.472, A.add)
    for out, z in ((LD0, 16), (LD2, 8)):
        t0, t1 = new("ka%d" % z, 9), new("kb%d" % z, 9)
        ts(t0, k, (1.0 - 18 * z) / z, A.mult)
        tt(t1, t0, j, A.add)
        ts(out, t1, float(z), A.mult)
    ts(LN, vw("li", 0, 18), 0.5, A.mult, KN, A.add)
    def away(at, m, c):
        a0, a1 = vw("ab", at, at + m), vw("ab", at + m, at + 2 * m)
        act(a0, vw("icp", 0, m), ACT.Abs, scale=-4.0, bias=c)
        scan(a1, a0, vw("dep", 0, m), 0.0, A.max, A.subtract)
        return a1[1]

    for b, weight in enumerate((4096.0, P112)):
        at = away(324 * b, 162, vw("pc", C2[1] + b, C2[1] + b + 1))
        ts(vw("cone0", b, 648, 4), vw("ab", at, at + 162), vw("pc", N0[1] + b, N0[1] + b + 1), A.is_le, weight, A.mult)
    quant("cone0", vw("cone0", 0, 648))
    at = away(648, 180, C8)
    for b, weight in enumerate((4096.0, P112)):
        ts(vw("cone1", b, 648, 4), vw("ab", at + 18 * b, at + 18 * b + 162), N2, A.is_le, weight, A.mult)
    quant("cone1", vw("cone1", 0, 648))
    FORMS = {"deep": (0, 72, 4), "nat": (198, 4, 64), "flat": (396, 4, 0)}
    for at, per, each in FORMS.values():
        if each:
            iota(vw("bc", at, at + 162), [[-each, 18], [per, 9]], 17 * each)
            sfill(vw("bc", at + 162, at + 180), float(-per - each))
            sfill(vw("bc", at + 180, at + 198), float(each - per))
        else:
            sfill(vw("bc", at + 162, at + 198), float(-per))
    PROG = {"x2t": (0, 4), "in": (144, 4), "top": (288, 4), "low": (432, 4), "x2b": (576, 5)}

    def slot(buf, name, s):
        at, steps = PROG[name]
        return vw(buf, at + s, at + 36 * steps, steps)

    for name, (at, steps) in PROG.items():
        labels.extend((buf, at, at + 36 * steps, buf + name) for buf in "pm")
    up, down, rows, edge = new("up"), new("down"), new("rows"), new("edge")
    iota(up, [[32, 18], [-16, 2]], 0)
    iota(down, [[-2, 18], [288, 2]], 0)
    iota(rows, [[4, 18], [-288, 2]], 504)
    act(edge, rows, bias=KB)
    act(slot("p", "top", 2), down, scale=1.0 / 9, bias=B2)
    act(slot("p", "top", 3), up, bias=B3)
    tab = [new("tab%d" % i) for i in range(7)]
    iota(tab[0], [[64, 18], [0, 2]], 64)
    iota(tab[3], [[96, 18], [-16, 2]], -628)
    act(tab[1], tab[3], bias=B4)
    iota(tab[6], [[32, 18], [16, 2]], -416)
    act(tab[5], tab[6], bias=K16)
    sfill(vw("win1", 0, 16), 0.0)
    iota(tab[4], [[-32, 18], [48, 2]], 1412)
    act(tab[2], tab[4], bias=B8)
    act(slot("p", "x2t", 2), tab[0], scale=-0.5, bias=1120.0)
    iota(slot("p", "x2b", 2), [[-32, 18], [0, 2]], 1088)
    sfill(vw("m", 290, 576, 4), 1.0 / 18)
    for (out, val), e in zip(((slot("m", "x2t", 1), -2.0), (slot("m", "x2b", 1), -2.0), (vw("m", 0, 288, 4), 0.0), (vw("m", 288, 576, 4), 0.0),
                              (slot("m", "x2b", 0), 0.0), (slot("m", "in", 1), 1.0), (slot("p", "in", 3), 0.0),
                              (vw("m", 289, 576, 4), 544.0 * 18), (slot("m", "top", 3), 1.0)), O["fill"]):
        sfill(out, val, e)

    quant("u", vw("ub", 0, 512))
    pick("up", "u", 128, LU)

    def sums(r):
        i = min(r, 1)
        for b in range(2):
            mm(4 + b, "x%d" % r if r else "d0", 16 * b, "up", 0, 128)["name"] = "score%d:%d" % (r, b)
        for b in range(2):
            out, src = vw("rich", b, 512, 4), vw("ps", 512 * (4 + b), 512 * (4 + b) + 128)
            if b == 1:
                act(out, src, ACT.Sign, bias=-1e-37)
            else:
                ts(out, src, 0.0, A.is_gt, 0.5, A.subtract)
            ops[-1]["name"] = "rich%d:%d" % (r, b)
        quant("rich", vw("rich", 0, 512))["name"] = "q_rich%d:0" % r
        mm(4, "rich", 0, "cone%d" % i, 0, 162)["name"] = "sums%d:0" % r

    def reach(form, outs, r=""):
        at = FORMS[form][0]
        m, f = new("m" + form + r, 162), new("f" + form + r, 18)
        caps = vw("bc", at, at + 162) if FORMS[form][2] else vw("dep", 0, 162)
        scan(m, vw("ps", 2048, 2048 + 162), caps, 5000.0, A.max, A.min)
        scan(f, vw("bc", at + 162, at + 180), step(m, 8, 9), -1000.0, A.add, A.max)
        for out in outs:
            scan(out, vw("bc", at + 180, at + 198), vw("wf", f[2] - 1, f[1] - 1, -1), -1000.0, A.add, A.max)

    def run(name, terms=None):
        at, steps = PROG[name]
        y, pt = new("run" + name, 36 * steps), PROG[terms or name][0]
        scan(y, vw("m", at, at + 36 * steps), vw("p", pt, pt + 36 * steps), 0.0, A.mult, A.add)
        return step(y, steps - 1, steps)

    def to_off(y, base, label):
        out = new(label, 36, "off")
        ts(out, y, base, A.add)
        return out

    def tops_out(r, lst, w):
        pick("d%d" % r, "x%d" % r, w, lst)
        send(r, [(vw("q_d%d" % r, 0, 144), vw("q_l%d" % r, 0, 144))])
        send(r, [(vw("s_d%d" % r, 0, 144), vw("s_l%d" % r, 0, 144))])

    def slots_out(r):
        o, a = "o%d" % r, new("adeep%d" % r, 18)
        reach("deep", [a], str(r))
        for h in range(2):
            ts(vw(o, h, 36, 2), a, KB, A.add, 504.0 - 288 * h, A.add)
        send(r, [(vw(o, 0, 36), vw("l" + o, 0, 36))])
        return a

    quant("x0", vw("x0", 0, 1152))
    tops_out(0, LD0, 288)
    sums(0)
    slots_out(0)
    n0, o1, near = new("n0", 18), new("ox1t", 36, "off"), new("near")
    reach("nat", [n0])
    unpack("t0", "x0", 0, 288, "src0", 0)
    quant("f0", vw("src0", 0, 1152))
    unpack("f0", "f0", 0, 288, "src1", 0)
    unpack("w0", "l0", 0, 144, "win", 576)
    for h in range(2):
        ts(step(o1, h, 2), n0, K16, A.add, 16.0 * h, A.add)
        act(step(near, h, 2), n0, bias=(KC, KD)[h])
    gather("x1t", vw("x1", 0, 576), vw("src0", 0, 1152), o1)
    quant("x1", vw("x1", 0, 576))
    send(1, [(vw("q_x1", 0, 144), vw("q_l1", 0, 144))])
    send(1, [(vw("s_x1", 0, 144), vw("s_l1", 0, 144))])
    sums(1)
    n1 = new("n1")
    reach("flat", [step(n1, h, 2) for h in range(2)])
    a1, z1, cut = new("a1"), new("z1"), slot("m", "in", 3)
    for h in range(2):
        ts(step(cut, 4 * h, 8), step(n1, h, 2), J4, A.add, 430.0 - 16 * h, A.is_ge)
        ts(vw("o1", 36 + h, 72, 2), step(n1, h, 2), J4, A.subtract, 30.0 - 16 * h, A.add)
    tt(a1, n1, tab[5], A.add)
    tt(z1, a1, cut, A.mult)
    cp(vw("o1", 0, 36), z1)
    send(1, [(vw("o1", 0, 72), vw("lo1", 0, 72))])
    gather("b0", vw("b0", 0, 576), vw("win", 0, 1152), vw("lo0", 0, 36))
    quant("b0", vw("b0", 0, 576))
    unpack("h0", "b0", 0, 144, "h0", 0, True)
    quant("h0", vw("h0", 0, 576))
    unpack("dh0", "h0", 0, 144, "src1", 1152)

    deep, far, got = new("deep"), new("far"), new("got")
    tt(deep, tab[0], near, A.subtract)
    for h, c in enumerate((CA, CB)):
        ts(step(got, h, 2), vw("lo0", h, 36, 2), 1.0 / 18, A.mult, c, A.add)
    tt(far, got, deep, A.add)

    def through(name, a):
        tt(slot("m", name, 2), a, far, A.is_ge)
        tt(slot("m", name, 3), a, deep, A.is_ge)

    tt(slot("p", "x2t", 1), near, tab[1], A.add)
    for s in (0, 3):
        tt(slot("p", "x2t", s), n1, near, A.add)
    through("x2t", n1)
    gather("x2t", vw("x2", 0, 576), vw("src1", 0, 1728), to_off(run("x2t"), 0.0, "ox2t"))
    quant("x2", vw("x2", 0, 576))
    unpack("w1", "l1", 0, 144, "win1", 16)
    gather("b1", vw("b1", 0, 576), vw("win1", 0, 592), vw("lo1", 0, 36))
    quant("b1", vw("b1", 0, 576))
    low = new("low")
    act(low, n1, bias=32.0)
    through("x2b", low)
    for s, more in ((0, 32.0), (1, 0.0), (3, 32.0)):
        act(slot("p", "x2b", s), slot("p", "x2t", s), bias=more)
    act(slot("m", "x2b", 4), cut, scale=-1.0, bias=1.0)
    act(slot("p", "in", 0), n1, ACT.Copy)
    tt(slot("p", "in", 1), tab[2], near, A.subtract)
    for h, c in enumerate((B6, B7)):
        act(step(slot("p", "in", 2), 4 * h, 8), step(near, h, 2), bias=c)

    tops_out(2, LD2, 144)
    sums(2)
    a2 = slots_out(2)
    for h in range(2):
        act(step(slot("p", "top", 1), 4 * h, 8), a2, ACT.Copy)
    tt(slot("p", "top", 0), slot("p", "top", 1), edge, A.is_gt)
    unpack("h1", "b1", 0, 144, "src1", 1728, True, True)
    unpack("t2t", "x2", 0, 144, "src2", 0)
    got = new("got1")
    cp(got, vw("lo1", 36, 72))
    tt(slot("m", "in", 2), n1, got, A.is_lt)
    act(slot("p", "x2b", 4), run("in"), ACT.Copy)
    gather("x2b", vw("x2", 576, 1152), vw("src1", 0, 2304), to_off(run("x2b"), 0.0, "ox2b"))
    quant("x2", vw("x2", 576, 1152), 144)
    unpack("w2", "l2", 0, 144, "win", 576)
    unpack("t2b", "x2", 144, 144, "src2", 576)
    dma("y", T.vb[:], T.v[:], [vw(O["vat"], 0, 36)] if O["vat"] else [], [vw("vb", 0, 512)], 131072)
    quant("v", vw("vb", 0, 512))
    ts(vw("li", 32, 50), a2, 1.0 / 72, A.mult, -0.472, A.add)
    cp(vw("oaf", 0, 18), vw("li", 32, 50))
    dma("y", T.oa[:], T.oaf[0:128:16, :], [vw("oaf", 0, 18)], [], 0)
    gather("b2", vw("b2", 0, 576), vw("win", 0, 1152), vw("lo2", 0, 36))
    quant("b2", vw("b2", 0, 576))
    unpack("h2", "b2", 0, 144, "src2", 1152, True)
    got = new("got2")
    ts(got, vw("lo2", 0, 36), 36.0, A.add)
    tt(slot("m", "low", 3), slot("p", "top", 1), got, A.is_lt)

    for i, (key, lst) in enumerate((("x3t", to_off(run("top"), 0.25, "ox3t")), ("x3b", to_off(run("low", "top"), 576.25, "ox3b")))):
        gather(key, vw("x3", 576 * i, 576 * i + 576), vw("src2", 0, 1152 + 576 * i), lst)
        quant("x3", vw("x3", 576 * i, 576 * i + 576), 144 * i)
        mm(4 + i, "v", 0, "x3", 144 * i, 144)
        src, out = vw("ps", 512 * (4 + i), 512 * (4 + i) + 144), T.yb[:, :, 8 * i:8 * i + 8]
        if O["y"][i] == "v":
            op("v", vdur(144), lambda q, s=src, o=out: q.tensor_copy(o, ap(s)), [src], [vw("yb", i, i + 1)])
        else:
            op("s", vdur(144), lambda q, s=src, o=out: q.activation(o, ap(s), ACT.Copy), [src], [vw("yb", i, i + 1)])
    for a, b in ((0, 10), (10, 18)):
        pick("last", "x3", 288, vw("lu", LN[1] + a, LN[1] + b), 16 * a)
        dma("y", T.oc[:, 64 * a:64 * b], T.q_last[:, 16 * a:16 * b].bitcast(dt.uint8), [vw("q_last", 16 * a, 16 * b)], [], 8192 * (b - a))
    for k in range(4):
        dma(O["out"][k], T.osc[4 * k:4 * k + 4, :], T.s_last[32 * k:32 * k + 4, :], [vw("s_last", 0, 288)], [], 0)
    dma(O["out"][4], T.y[:], T.yb[:], [vw("yb", 0, 2)], [], 150000)
    return ops


def depend(ops):
    last = {}
    for o in ops:
        deps = set()
        for v, w in [(v, False) for v in o["r"]] + [(v, True) for v in o["w"]]:
            bank = v[0] == "ps"
            key = (v[0], v[1] // 512) if bank else v[0]
            cs = None if bank else frozenset(cols(v))
            for (j, cj, wj) in last.get(key, ()):
                if j == o["id"]:
                    continue
                if bank:
                    if ops[j]["eng"] != o["eng"] or w or wj:
                        deps.add(j)
                elif (w or wj) and not cs.isdisjoint(cj):
                    deps.add(j)
            last.setdefault(key, []).append((o["id"], cs, w))
        o["deps"] = deps


def place(busy, t, dur):
    for a, b in busy:
        if t < b and t + dur > a:
            t = b
    busy.append((t, t + dur))
    busy.sort()
    return t


def order(ops, C=COST, late=None):
    late = LATE if late is None else late
    named = {o["name"]: o for o in ops}
    for o in ops:
        o["behind"] = set()
    for row in late.get("rows", ROWS):
        row = [named[x if ":" in x else x + ":0"] for x in row.split()]
        for e in "vstgy":
            mine = [o for o in row if o["eng"] == e]
            for a, b in zip(mine, mine[1:]):
                b["behind"].add(a["id"])
    after = [[] for o in ops]
    for o in ops:
        o["ahead"], o["need"] = None, len(o["deps"] | o["behind"])
        for j in o["deps"] | o["behind"]:
            after[j].append(o)

    def ahead(o):
        if o["ahead"] is None:
            tail = o["lat"] + o.get("pre", 0.0) + o.get("wire", 0.0)
            o["ahead"] = o["dur"] + late.get(o["name"] + "+", 0.0) + max(
                [tail] + [ahead(x) + (tail + C["wake"] if o["id"] in x["deps"] else 0.0) for x in after[o["id"]]])
        return o["ahead"]

    for o in reversed(ops):
        ahead(o)
    free, done, wire, seq, first = {}, {}, [], [], [C["first"]]
    ready = [o for o in ops if not o["need"]]
    for o in ready:
        o["from"] = late.get(o["name"], 0.0)
    while ready:
        o = min(ready, key=lambda o: (max(o["from"], free.get(o["eng"], 0.0)), -o["ahead"]))
        t = max(o["from"], free.get(o["eng"], 0.0))
        o = max([x for x in ready if x["eng"] == o["eng"] and x["from"] <= t + C["patience"] * o["dur"]], key=lambda x: x["ahead"])
        t = free[o["eng"]] = max(t, o["from"]) + o["dur"] + (first.pop() if o["kind"] == "r" and first else 0.0)
        if o["kind"] != "c":
            t = place(wire, t + o["pre"], o["wire"]) + o["wire"] + o["lat"]
        done[o["id"]] = t
        seq.append(o)
        ready.remove(o)
        for x in after[o["id"]]:
            x["need"] -= 1
            if not x["need"]:
                x["from"] = max([late.get(x["name"], 0.0)] + [done[j] + C["wake"] for j in x["deps"]])
                ready.append(x)
    return seq


def settle(ops, seq, C=COST):
    first = next(o for o in seq if o["kind"] == "r")
    after = [[] for o in ops]
    for o in ops:
        o["hold"] = o["dur"] * (C["busy"] if o["kind"] == "c" else 1.0) + (C["first"] if o is first else 0.0)
        o["tail"] = o["lat"] + o.get("pre", 0.0) + o.get("wire", 0.0)
        for j in o["deps"] | o["behind"]:
            after[j].append(o)
    for sweep in range(2):
        busy, back = {}, {}
        for o in reversed(seq):
            t = max([o["tail"]] + [back[x["id"]] + (C["pause"] + o["tail"] if o["id"] in x["deps"] else 0.0) for x in after[o["id"]]])
            if o is first:
                t = max([t] + [back[x["id"]] for x in ops if x["kind"] == "r" and x is not o])
            back[o["id"]] = place(busy.setdefault(o["eng"], []), t, o["hold"]) + o["hold"]
        busy, start, done = {}, {}, {}
        for o in sorted(seq, key=lambda o: -back[o["id"]]):
            t = max([start.get(first["id"], 0.0) if o["kind"] == "r" else 0.0] + [done[j] + C["pause"] for j in o["deps"]]
                    + [start[j] + ops[j]["hold"] for j in o["behind"]])
            start[o["id"]] = t = place(busy.setdefault(o["eng"], []), t, o["hold"])
            t += o["hold"]
            if o["kind"] != "c":
                t = place(busy.setdefault("wire", []), t + o["pre"], o["wire"]) + o["wire"] + o["lat"]
            done[o["id"]] = t
        seq = sorted(seq, key=lambda o: start[o["id"]])
    return seq


def rank_program(g, core, T, topo):
    rank = T.rank_of(core)
    if rank is None:
        return
    ops = plan(T, topo, core, rank)
    depend(ops)
    for o in ops:
        if o["kind"] == "r":
            o["lat"], o["wire"] = o["lat"] * COST["slow"], o["wire"] * COST["slow"]
    seq = settle(ops, order(ops))
    queue = {"v": g.vector, "s": g.scalar, "t": g.tensor, "g": g, "y": g.sync}
    known, count = {e: {} for e in queue}, {e: 0 for e in queue}
    for i, o in enumerate(seq):
        o["place"] = i
        if o["kind"] == "c":
            count[o["eng"]] += 1
            o["src"], o["at"] = o["eng"], count[o["eng"]]
        else:
            o["src"], o["at"] = ("x", o["id"]), 1
        kn = known[o["eng"]]
        need = {}
        for j in o["deps"]:
            d = ops[j]
            if o["acc"] and d["eng"] == "t":
                continue
            if kn.get(d["src"], 0) < d["at"] and need.get(d["src"], {"at": 0})["at"] < d["at"]:
                need[d["src"]] = d
        waits = []
        for d in sorted(need.values(), key=lambda d: -d["place"]):
            if kn.get(d["src"], 0) < d["at"]:
                waits.append(d)
                d["inc"] = True
                kn[d["src"]] = d["at"]
                if d["kind"] != "r":
                    for s, a in d["knew"].items():
                        kn[s] = max(kn.get(s, 0), a)
        o["waits"], o["knew"] = waits[::-1], dict(kn)
    total, nd, nr, sent = {e: 0 for e in queue}, 0, 0, 0
    for o in ops:
        if o["kind"] == "r":
            o["sem"], o["val"] = T.sem["ar%d" % nr], o["n"]
            nr += 1
        elif o["kind"] == "d":
            o["sem"], o["val"] = T.sem["dm%d" % nd], 16
            nd += 1
    for o in seq:
        q = queue[o["eng"]]
        for d in o["waits"]:
            q.wait_ge(d["sem"], d["val"])
        if o["kind"] == "r":
            o["fn"](q, o["sem"], T.sem.sent)
            sent += o["n"]
        elif o["kind"] == "d":
            o["fn"](q).then_inc(o["sem"], 16)
        elif o.get("inc"):
            total[o["eng"]] += 1
            o["sem"], o["val"] = T.sem["c" + o["eng"]], total[o["eng"]]
            o["fn"](q).then_inc(o["sem"], 1)
        else:
            o["fn"](q)
    g.wait_ge(T.sem.sent, sent)
    for o in seq:
        if o["kind"] == "d" and not o.get("inc"):
            queue[o["eng"]].wait_ge(o["sem"], 16)
